import numpy as np
import ml_dtypes


def mxq(x, axis, fmt="e4m3"):
    dtype, down = {"e4m3": (ml_dtypes.float8_e4m3fn, 7), "e5m2": (ml_dtypes.float8_e5m2, 14)}[fmt]
    v = np.moveaxis(np.asarray(x, np.float32).astype(ml_dtypes.bfloat16).astype(np.float64), axis, -1)
    blocks = v.reshape(v.shape[:-1] + (-1, 32))
    amax = np.abs(blocks).max(-1, keepdims=True)
    byte = np.maximum(np.where(amax > 0, np.frexp(amax)[1] - 1 + 127, 0) - down, 1)
    scale = np.exp2(byte - 127.0)
    codes = (blocks / scale).astype(np.float32).astype(dtype).astype(np.float64)
    return np.moveaxis((codes * scale).reshape(v.shape), -1, axis)


WIDE = False


def mx_kscale(k):
    if not WIDE:
        return np.ones(k)
    levels = np.array([10, -10, 5, -5, 0])
    if k % 512:
        return np.exp2(np.random.permutation(np.resize(levels, k // 32))).repeat(32)
    a = np.empty((k // 512, 16))
    for p in range(k // 512):
        a[p, :8] = np.random.permutation(np.resize(levels, 8))
        for g in range(8):
            far = levels[np.abs(levels - a[p, g]) >= 10]
            a[p, g + 8] = far[np.random.randint(len(far))]
    return np.exp2(a.ravel()).repeat(32)


def f64(x):
    return np.asarray(x).astype(np.float64)


def striped(idx):
    return np.tile(np.asarray(idx).reshape(-1, 16).T, (8, 1)).astype(np.uint16)


def unstriped(offs):
    return offs[:16].T.reshape(-1).astype(np.int64)


def striped8(idx):
    return np.asarray(idx).reshape(8, -1, 16).transpose(0, 2, 1).reshape(128, -1).astype(np.uint16)


def unstriped8(offs):
    return offs.reshape(8, 16, -1).transpose(0, 2, 1).reshape(8, -1).astype(np.int64)


def pick8(x, idx, run):
    r = np.arange(len(x))
    return x[r[:, None], idx[r % (8 * run) // run]]


E2M1 = np.array([0.0, 0.5, 1.0, 1.5, 2.0, 3.0, 4.0, 6.0, -0.0, -0.5, -1.0, -1.5, -2.0, -3.0, -4.0, -6.0])


def pack_weight(w, fmt):
    k, n = w.shape
    w = f64(np.asarray(w, np.float32).astype(ml_dtypes.bfloat16)).reshape(k // 32, 32, n)
    amax = np.abs(w).max(1)
    if fmt == "e4m3":
        byte = np.frexp(amax)[1] - 1 + 127 - 7
    else:
        mant, ex = np.frexp(amax / 6.0)
        byte = np.where(mant > 0.5, ex, ex - 1) + 127
    byte = np.clip(np.where(amax > 0, byte, 1), 1, 254)
    scaled = (w * np.exp2(127.0 - byte)[:, None, :]).reshape(k, n).astype(np.float32)
    by_word = np.ascontiguousarray(scaled.reshape(k // 512, 128, 4, n).transpose(0, 1, 3, 2))
    if fmt == "e4m3":
        words = by_word.astype(ml_dtypes.float8_e4m3fn).view(np.uint8)
    else:
        c = by_word.astype(ml_dtypes.float4_e2m1fn).view(np.uint8) & 0xF
        words = (c[..., 0::2] | (c[..., 1::2] << 4)).reshape(k // 512, 128, 2 * n)
    return np.ascontiguousarray(words), np.ascontiguousarray(byte.astype(np.uint8).reshape(k // 512, 16, n))


def unpack_weight(words, scales, fmt):
    g, _, n = scales.shape
    words = np.ascontiguousarray(words).reshape(g, 128, n, -1)
    if fmt == "e4m3":
        vals = words.view(ml_dtypes.float8_e4m3fn).astype(np.float64)
    else:
        nib = np.empty((g, 128, n, 4), np.uint8)
        nib[..., 0::2] = words & 0xF
        nib[..., 1::2] = words >> 4
        vals = E2M1[nib]
    vals = vals * np.repeat(np.exp2(scales.astype(np.float64) - 127.0), 8, axis=1)[..., None]
    return vals.transpose(0, 1, 3, 2).reshape(g * 512, n)


D, T, I, C, Q, E = 512, 2048, 512, 1024, 128, 512


def setup_inputs():
    n = np.random.standard_normal
    idx = np.random.permutation(T)[:I]
    idx2 = np.stack([np.random.randint(0, C, I) for _ in range(8)])
    fd = mx_kscale(D)
    fi = mx_kscale(I)
    keysp = pack_weight(n((D, T)) / fd[:, None], "e4m3")
    return {
        "query": (n((D, Q)) * 0.25 / np.sqrt(D) * fd[:, None]).astype(np.float32),
        "keys_words": keysp[0],
        "keys_scales": keysp[1],
        "vbook": (n((E, C))).astype(np.float32),
        "size": (np.random.uniform(0.5, 2.0, (1, I)) * fi).astype(np.float32),
        "vsc": (np.random.uniform(0.5, 2.0, (I, 1)) / fi[:, None]).astype(np.float32),
        "offs": striped(idx),
        "offs2": striped8(idx2),
    }


def reference(query, keys_words, keys_scales, vbook, size, vsc, offs, offs2):
    idx = unstriped(offs)
    idx2 = unstriped8(offs2)
    keysu = unpack_weight(keys_words, keys_scales, "e4m3")
    queryq = mxq(f64(query), 0, "e4m3")
    keysidxg = keysu[:, idx]
    a = queryq.T @ keysidxg
    p = np.exp(a - np.max(a, axis=1, keepdims=True))
    w = p * f64(size) / np.sum(p, axis=1, keepdims=True)
    wt = w.T
    v = pick8(f64(vbook), idx2, 64).T
    vv = v * f64(vsc)
    wtq = mxq(wt, 0, "e4m3")
    vvq = mxq(vv, 0, "e4m3")
    o = wtq.T @ vvq
    return o

@@ -1,0 +1,183 @@
+from contextlib import ExitStack
+
+import concourse.mybir as mybir
+from concourse.masks import make_identity
+
+D, T, I, C, Q, E = 512, 2048, 512, 1024, 128, 512
+FLOPS = 2 * Q * I * D + 2 * Q * I * E
+
+F32 = mybir.dt.float32
+BF16 = mybir.dt.bfloat16
+I32 = mybir.dt.int32
+U32 = mybir.dt.uint32
+U16 = mybir.dt.uint16
+U8 = mybir.dt.uint8
+FP8X4 = mybir.dt.float8_e4m3fn_x4
+ALU = mybir.AluOpType
+ACT = mybir.ActivationFunctionType
+AXIS = mybir.AxisListType
+
+P = 128
+PACK = 4
+HALVES = 2
+HP = P // HALVES
+
+
+def tile_attend_pqvalues_kernel(tc, query, keys_words, keys_scales, vbook, size, vsc, offs, offs2, out):
+    nc = tc.nc
+    with ExitStack() as ctx:
+        sb = ctx.enter_context(tc.tile_pool(name="sb", bufs=1))
+        ps = ctx.enter_context(tc.psum_pool(name="ps", bufs=1))
+
+        key_list = sb.tile([P, I // 16], U16, name="key_list")
+        code_lists = sb.tile([P, I // 16], U16, name="code_lists")
+        vsc_col = sb.tile([P, PACK], F32, name="vsc_col")
+        size_col = sb.tile([P, PACK], F32, name="size_col")
+        books = [sb.tile([P, C], F32, name="book%d" % j) for j in range(PACK)]
+        key_words = sb.tile([P, T], I32, name="key_words")
+        key_bytes = sb.tile([P, T], U8, name="key_bytes")
+        q_raw = sb.tile([P, PACK, Q], F32, name="q_raw")
+        ident = sb.tile([P, P], F32, name="ident")
+        warm_out = sb.tile([P, 1], F32, name="warm_out")
+
+        nc.vector.memset(key_bytes[:].bitcast(I32), 0)
+        make_identity(nc, ident[:])
+
+        book_rows = vbook.rearrange("(p j) c -> j p c", j=PACK)
+        nc.scalar.dma_start(vsc_col[:], vsc.rearrange("(p t) o -> p (t o)", t=PACK))
+        nc.sync.dma_start(key_list[:], offs)
+        nc.sync.dma_start(books[0][:], book_rows[0])
+        nc.sync.dma_start(code_lists[:], offs2)
+        for quad in range(4):
+            nc.scalar.dma_start(
+                key_bytes[32 * quad : 32 * quad + 4, :].bitcast(I32),
+                keys_scales[0, 4 * quad : 4 * quad + 4, :].bitcast(I32),
+            )
+        nc.sync.dma_start(books[1][:], book_rows[1])
+        nc.sync.dma_start(q_raw[:], query.rearrange("(p j) q -> p j q", j=PACK))
+        nc.sync.dma_start(key_words[:], keys_words[0].rearrange("p n t -> p (n t)").bitcast(I32))
+        nc.gpsimd.dma_start(size_col[:], size.rearrange("o (p t) -> p (o t)", t=PACK))
+        nc.sync.dma_start(books[2][:], book_rows[2])
+        nc.sync.dma_start(books[3][:], book_rows[3])
+
+        def spread(col, name):
+            bank = ps.tile([P, PACK, P], F32, name=name)
+            for t in range(PACK):
+                nc.tensor.transpose(bank[:, t, :], col[:, t : t + 1].to_broadcast([P, P]), ident[:])
+            return bank
+
+        vsc_bank = spread(vsc_col, "vsc_bank")
+        vsc_row = sb.tile([P, I], F32, name="vsc_row")
+        nc.scalar.copy(vsc_row[:].rearrange("p (n t) -> p n t", t=PACK), vsc_bank[:].rearrange("p t n -> p n t"))
+        nc.scalar.activation(warm_out[:], vsc_row[:, 0:1], ACT.Exp, scale=0.0)
+
+        def turn(rows_bf16, name, tag):
+            words = rows_bf16[:].bitcast(F32)
+            bank = ps.tile([P, 2, P], F32, name=name + "_bank", tag=tag)
+            for u in range(2):
+                nc.tensor.transpose(bank[:, u, :], words[:, u : I // 2 : 2], ident[:])
+            return bank
+
+        v_woven = sb.tile([P, HALVES, PACK, HP * PACK], BF16, name="v_woven", align_bytes=64)
+        v_codes = sb.tile([P, HALVES, PACK, HP], U32, name="v_codes", align_bytes=64)
+        v_scales = sb.tile([P, HALVES, PACK, HP], U8, name="v_scales", align_bytes=64)
+
+        def values(j):
+            prod = sb.tile([P, I], F32, name="prod%d" % j)
+            nc.vector.tensor_tensor(prod[:], books[j][:].indirect(code_lists[:]), vsc_row[:], ALU.mult)
+            rounded = sb.tile([P, I], BF16, name="rounded%d" % j)
+            nc.scalar.copy(rounded[:], prod[:])
+            return turn(rounded, "v%d" % j, "vbank%d" % (j % 2))
+
+        def weave_values(j, bank):
+            nc.scalar.copy(
+                v_woven[:, :, j, :].bitcast(F32).rearrange("p h (r u) -> p h r u", u=2),
+                bank[:].rearrange("p u (h r) -> p h r u", h=HALVES),
+            )
+
+        def quantise_values(first, last):
+            for h in range(HALVES):
+                nc.vector.quantize_mx(
+                    out=v_codes[:, h, first:last, :].rearrange("p j r -> p (j r)").bitcast(FP8X4),
+                    scales=v_scales[:, h, first:last, :].rearrange("p j r -> p (j r)"),
+                    in_=v_woven[:, h, first:last, :].rearrange("p j r -> p (j r)"),
+                )
+
+        def quantise(woven, name):
+            codes = sb.tile([P, P], U32, name=name + "_codes", align_bytes=64)
+            scales = sb.tile([P, P], U8, name=name + "_scales", align_bytes=64)
+            nc.vector.quantize_mx(out=codes[:].bitcast(FP8X4), scales=scales[:], in_=woven[:])
+            return codes, scales
+
+        picked_bytes = sb.tile([P, I], U8, name="picked_bytes", align_bytes=64)
+        nc.vector.tensor_copy(picked_bytes[:], key_bytes[:].indirect(key_list[:]))
+        weave_values(0, values(0))
+        bank1 = values(1)
+
+        q_woven = sb.tile([P, Q * PACK], BF16, name="q_woven", align_bytes=64)
+        nc.scalar.copy(q_woven[:].rearrange("p (q j) -> p q j", j=PACK), q_raw[:].rearrange("p j q -> p q j"))
+        quantise_values(0, 1)
+        q_codes, q_scales = quantise(q_woven, "q")
+        weave_values(1, bank1)
+
+        picked_words = sb.tile([P, I], U32, name="picked_words", align_bytes=64)
+        nc.vector.tensor_copy(picked_words[:], key_words[:].bitcast(U32).indirect(key_list[:]))
+        size_bank = spread(size_col, "size_bank")
+        scores = ps.tile([P, I], F32, name="scores")
+        nc.tensor.matmul_mx(
+            out=scores[:],
+            lhsT=q_codes[:].bitcast(FP8X4),
+            lhsT_scale=q_scales[:],
+            rhs=picked_words[:].bitcast(FP8X4),
+            rhs_scale=picked_bytes[:],
+            start=True,
+            stop=True,
+        )
+        bank2 = values(2)
+
+        neg_max = sb.tile([P, 1], F32, name="neg_max", tag="book2")
+        nc.vector.tensor_reduce(neg_max[:], scores[:], AXIS.X, ALU.max, negate=True)
+        probs = sb.tile([P, I], F32, name="probs")
+        row_sum = sb.tile([P, 1], F32, name="row_sum")
+        nc.scalar.activation(probs[:], scores[:], ACT.Exp, bias=neg_max[:], accum_out=row_sum[:])
+        weave_values(2, bank2)
+
+        bank3 = values(3)
+
+        inv_sum = sb.tile([P, 1], F32, name="inv_sum", tag="book3")
+        nc.vector.reciprocal(inv_sum[:], row_sum[:])
+        weights = sb.tile([P, I], BF16, name="weights")
+        nc.vector.scalar_tensor_tensor(
+            weights[:].rearrange("p (n t) -> p n t", t=PACK),
+            probs[:].rearrange("p (n t) -> p n t", t=PACK),
+            inv_sum[:],
+            size_bank[:].rearrange("p t n -> p n t"),
+            ALU.mult,
+            ALU.mult,
+        )
+        quantise_values(1, 3)
+        weave_values(3, bank3)
+        w_bank = turn(weights, "w", "vsc_bank")
+        w_woven = sb.tile([P, Q * PACK], BF16, name="w_woven", align_bytes=64)
+        nc.vector.tensor_copy(
+            w_woven[:].bitcast(F32).rearrange("p (r u) -> p r u", u=2), w_bank[:].rearrange("p u r -> p r u")
+        )
+        quantise_values(3, 4)
+        w_codes, w_scales = quantise(w_woven, "w")
+
+        for h in range(HALVES):
+            sums = ps.tile([P, PACK, HP], F32, name="sums%d" % h)
+            nc.tensor.matmul_mx(
+                out=sums[:].rearrange("q j r -> q (j r)"),
+                lhsT=w_codes[:].bitcast(FP8X4),
+                lhsT_scale=w_scales[:],
+                rhs=v_codes[:, h, :, :].rearrange("p j r -> p (j r)").bitcast(FP8X4),
+                rhs_scale=v_scales[:, h, :, :].rearrange("p j r -> p (j r)"),
+                start=True,
+                stop=True,
+            )
+            result = sb.tile([P, E // HALVES], F32, name="result%d" % h)
+            copy = (nc.vector.tensor_copy, nc.scalar.copy)[h]
+            copy(result[:].rearrange("q (r j) -> q r j", j=PACK), sums[:].rearrange("q j r -> q r j"))
+            queue = (nc.sync, nc.scalar)[h]
+            queue.dma_start(out[:, h * (E // HALVES) : (h + 1) * (E // HALVES)], result[:])

@@ -29,36 +29,44 @@ def tile_attend_pqvalues_kernel(tc, query, keys_words, keys_scales, vbook, size,
         sb = ctx.enter_context(tc.tile_pool(name="sb", bufs=1))
         ps = ctx.enter_context(tc.psum_pool(name="ps", bufs=1))
 
+        def tile(shape, dtype, name, slot=None):
+            return sb.tile(shape, dtype, name=name, tag=slot or name, align_bytes=64)
+
         key_list = sb.tile([P, I // 16], U16, name="key_list")
         code_lists = sb.tile([P, I // 16], U16, name="code_lists")
-        vsc_col = sb.tile([P, PACK], F32, name="vsc_col")
-        size_col = sb.tile([P, PACK], F32, name="size_col")
-        books = [sb.tile([P, C], F32, name="book%d" % j) for j in range(PACK)]
-        key_words = sb.tile([P, T], I32, name="key_words")
-        key_bytes = sb.tile([P, T], U8, name="key_bytes")
-        q_raw = sb.tile([P, PACK, Q], F32, name="q_raw")
-        ident = sb.tile([P, P], F32, name="ident")
-        warm_out = sb.tile([P, 1], F32, name="warm_out")
+        vsc_col = tile([P, PACK], F32, "vsc_col")
+        key_words = tile([P, T], I32, "key_words")
+        key_bytes = tile([P, T], U8, "key_bytes")
+        q_raw = tile([P, PACK, Q], F32, "q_raw")
+        ident = tile([P, P], F32, "ident")
+        warm_out = tile([P, 1], F32, "warm_out")
 
         nc.vector.memset(key_bytes[:].bitcast(I32), 0)
         make_identity(nc, ident[:])
 
         book_rows = vbook.rearrange("(p j) c -> j p c", j=PACK)
+        books = []
+
+        def load_book(j, slot):
+            book = tile([P, C], F32, "book%d" % j, slot)
+            nc.sync.dma_start(book[:], book_rows[j])
+            books.append(book)
+
         nc.scalar.dma_start(vsc_col[:], vsc.rearrange("(p t) o -> p (t o)", t=PACK))
-        nc.sync.dma_start(key_list[:], offs)
-        nc.sync.dma_start(books[0][:], book_rows[0])
-        nc.sync.dma_start(code_lists[:], offs2)
+        size_col = tile([P, PACK], F32, "size_col")
+        nc.scalar.dma_start(size_col[:], size.rearrange("o (p t) -> p (o t)", t=PACK))
         for quad in range(4):
             nc.scalar.dma_start(
                 key_bytes[32 * quad : 32 * quad + 4, :].bitcast(I32),
                 keys_scales[0, 4 * quad : 4 * quad + 4, :].bitcast(I32),
             )
-        nc.sync.dma_start(books[1][:], book_rows[1])
+        nc.scalar.activation(warm_out[:], ident[:, 0:1], ACT.Exp)
+        nc.sync.dma_start(code_lists[:], offs2)
+        nc.sync.dma_start(key_list[:], offs)
+        load_book(0, None)
+        load_book(1, None)
         nc.sync.dma_start(q_raw[:], query.rearrange("(p j) q -> p j q", j=PACK))
         nc.sync.dma_start(key_words[:], keys_words[0].rearrange("p n t -> p (n t)").bitcast(I32))
-        nc.gpsimd.dma_start(size_col[:], size.rearrange("o (p t) -> p (o t)", t=PACK))
-        nc.sync.dma_start(books[2][:], book_rows[2])
-        nc.sync.dma_start(books[3][:], book_rows[3])
 
         def spread(col, name):
             bank = ps.tile([P, PACK, P], F32, name=name)
@@ -67,62 +75,58 @@ def tile_attend_pqvalues_kernel(tc, query, keys_words, keys_scales, vbook, size,
             return bank
 
         vsc_bank = spread(vsc_col, "vsc_bank")
-        vsc_row = sb.tile([P, I], F32, name="vsc_row")
-        nc.scalar.copy(vsc_row[:].rearrange("p (n t) -> p n t", t=PACK), vsc_bank[:].rearrange("p t n -> p n t"))
-        nc.scalar.activation(warm_out[:], vsc_row[:, 0:1], ACT.Exp, scale=0.0)
+        vsc_row = tile([P, I], F32, "vsc_row")
+        nc.vector.tensor_copy(
+            vsc_row[:].rearrange("p (n t) -> p n t", t=PACK), vsc_bank[:].rearrange("p t n -> p n t")
+        )
+        load_book(2, "vsc_col")
 
-        def turn(rows_bf16, name, tag):
-            words = rows_bf16[:].bitcast(F32)
-            bank = ps.tile([P, 2, P], F32, name=name + "_bank", tag=tag)
+
+        def values(j, slot):
+            prod = tile([P, I], F32, "prod%d" % j, slot)
+            nc.vector.tensor_tensor(prod[:], books[j][:].indirect(code_lists[:]), vsc_row[:], ALU.mult)
+            rounded = tile([P, 2, P, 2], BF16, "rounded%d" % j)
+            nc.scalar.copy(rounded[:], prod[:].rearrange("p (n u e) -> p u n e", u=2, e=2))
+            bank = ps.tile([P, 2, P], F32, name="v%d_bank" % j, tag="vbank%d" % (j % 2))
             for u in range(2):
-                nc.tensor.transpose(bank[:, u, :], words[:, u : I // 2 : 2], ident[:])
+                words = rounded[:, u].rearrange("p n e -> p (n e)").bitcast(F32)
+                nc.tensor.transpose(bank[:, u, :], words, ident[:])
             return bank
 
-        v_woven = sb.tile([P, HALVES, PACK, HP * PACK], BF16, name="v_woven", align_bytes=64)
-        v_codes = sb.tile([P, HALVES, PACK, HP], U32, name="v_codes", align_bytes=64)
-        v_scales = sb.tile([P, HALVES, PACK, HP], U8, name="v_scales", align_bytes=64)
-
-        def values(j):
-            prod = sb.tile([P, I], F32, name="prod%d" % j)
-            nc.vector.tensor_tensor(prod[:], books[j][:].indirect(code_lists[:]), vsc_row[:], ALU.mult)
-            rounded = sb.tile([P, I], BF16, name="rounded%d" % j)
-            nc.scalar.copy(rounded[:], prod[:])
-            return turn(rounded, "v%d" % j, "vbank%d" % (j % 2))
-
-        def weave_values(j, bank):
+        def weave_values(woven, j, bank):
             nc.scalar.copy(
-                v_woven[:, :, j, :].bitcast(F32).rearrange("p h (r u) -> p h r u", u=2),
+                woven[:, :, j % 2, :].bitcast(F32).rearrange("p h (r u) -> p h r u", u=2),
                 bank[:].rearrange("p u (h r) -> p h r u", h=HALVES),
             )
 
-        def quantise_values(first, last):
+        def quantise_values(woven, first):
+            last = first + 2
             for h in range(HALVES):
                 nc.vector.quantize_mx(
                     out=v_codes[:, h, first:last, :].rearrange("p j r -> p (j r)").bitcast(FP8X4),
                     scales=v_scales[:, h, first:last, :].rearrange("p j r -> p (j r)"),
-                    in_=v_woven[:, h, first:last, :].rearrange("p j r -> p (j r)"),
+                    in_=woven[:, h, :, :].rearrange("p j r -> p (j r)"),
                 )
 
-        def quantise(woven, name):
-            codes = sb.tile([P, P], U32, name=name + "_codes", align_bytes=64)
-            scales = sb.tile([P, P], U8, name=name + "_scales", align_bytes=64)
+        def quantise(woven, name, slot):
+            codes = tile([P, P], U32, name + "_codes", slot)
+            scales = tile([P, P], U8, name + "_scales")
             nc.vector.quantize_mx(out=codes[:].bitcast(FP8X4), scales=scales[:], in_=woven[:])
             return codes, scales
 
-        picked_bytes = sb.tile([P, I], U8, name="picked_bytes", align_bytes=64)
-        nc.vector.tensor_copy(picked_bytes[:], key_bytes[:].indirect(key_list[:]))
-        weave_values(0, values(0))
-        bank1 = values(1)
-
-        q_woven = sb.tile([P, Q * PACK], BF16, name="q_woven", align_bytes=64)
+        q_woven = tile([P, Q * PACK], BF16, "q_woven")
         nc.scalar.copy(q_woven[:].rearrange("p (q j) -> p q j", j=PACK), q_raw[:].rearrange("p j q -> p q j"))
-        quantise_values(0, 1)
-        q_codes, q_scales = quantise(q_woven, "q")
-        weave_values(1, bank1)
+        load_book(3, "q_raw")
+        woven01 = tile([P, HALVES, 2, HP * PACK], BF16, "woven01")
+        weave_values(woven01, 0, values(0, None))
+        bank1 = values(1, None)
+        picked_bytes = tile([P, I], U8, "picked_bytes", "book0")
+        nc.vector.tensor_copy(picked_bytes[:], key_bytes[:].indirect(key_list[:]))
+        q_codes, q_scales = quantise(q_woven, "q", "book1")
+        weave_values(woven01, 1, bank1)
 
-        picked_words = sb.tile([P, I], U32, name="picked_words", align_bytes=64)
+        picked_words = tile([P, I], U32, "picked_words", "key_bytes")
         nc.vector.tensor_copy(picked_words[:], key_words[:].bitcast(U32).indirect(key_list[:]))
-        size_bank = spread(size_col, "size_bank")
         scores = ps.tile([P, I], F32, name="scores")
         nc.tensor.matmul_mx(
             out=scores[:],
@@ -133,37 +137,43 @@ def tile_attend_pqvalues_kernel(tc, query, keys_words, keys_scales, vbook, size,
             start=True,
             stop=True,
         )
-        bank2 = values(2)
+        bank2 = values(2, "q_woven")
+        size_bank = spread(size_col, "size_bank")
 
-        neg_max = sb.tile([P, 1], F32, name="neg_max", tag="book2")
+        neg_max = tile([P, 1], F32, "neg_max")
         nc.vector.tensor_reduce(neg_max[:], scores[:], AXIS.X, ALU.max, negate=True)
-        probs = sb.tile([P, I], F32, name="probs")
-        row_sum = sb.tile([P, 1], F32, name="row_sum")
+        probs = tile([P, I], F32, "probs")
+        row_sum = tile([P, 1], F32, "row_sum")
         nc.scalar.activation(probs[:], scores[:], ACT.Exp, bias=neg_max[:], accum_out=row_sum[:])
-        weave_values(2, bank2)
 
-        bank3 = values(3)
+        woven23 = tile([P, HALVES, 2, HP * PACK], BF16, "woven23", "neg_max")
+        weave_values(woven23, 2, bank2)
+        bank3 = values(3, "key_bytes")
 
-        inv_sum = sb.tile([P, 1], F32, name="inv_sum", tag="book3")
+        inv_sum = tile([P, 1], F32, "inv_sum", "q_raw")
         nc.vector.reciprocal(inv_sum[:], row_sum[:])
-        weights = sb.tile([P, I], BF16, name="weights")
-        nc.vector.scalar_tensor_tensor(
-            weights[:].rearrange("p (n t) -> p n t", t=PACK),
-            probs[:].rearrange("p (n t) -> p n t", t=PACK),
-            inv_sum[:],
-            size_bank[:].rearrange("p t n -> p n t"),
-            ALU.mult,
-            ALU.mult,
-        )
-        quantise_values(1, 3)
-        weave_values(3, bank3)
-        w_bank = turn(weights, "w", "vsc_bank")
-        w_woven = sb.tile([P, Q * PACK], BF16, name="w_woven", align_bytes=64)
-        nc.vector.tensor_copy(
+        w_bank = ps.tile([P, 2, P], F32, name="w_bank", tag="vsc_bank")
+        for u in range(2):
+            weights = tile([P, P, 2], BF16, "weights%d" % u)
+            nc.vector.scalar_tensor_tensor(
+                weights[:],
+                probs[:].rearrange("p (n u e) -> p u n e", u=2, e=2)[:, u],
+                inv_sum[:],
+                size_bank[:, 2 * u : 2 * u + 2, :].rearrange("p e n -> p n e"),
+                ALU.mult,
+                ALU.mult,
+            )
+            nc.tensor.transpose(w_bank[:, u, :], weights[:].rearrange("p n e -> p (n e)").bitcast(F32), ident[:])
+        weave_values(woven23, 3, bank3)
+        v_codes = tile([P, HALVES, PACK, HP], U32, "v_codes", "probs")
+        v_scales = tile([P, HALVES, PACK, HP], U8, "v_scales")
+        quantise_values(woven01, 0)
+        w_woven = tile([P, Q * PACK], BF16, "w_woven")
+        nc.scalar.copy(
             w_woven[:].bitcast(F32).rearrange("p (r u) -> p r u", u=2), w_bank[:].rearrange("p u r -> p r u")
         )
-        quantise_values(3, 4)
-        w_codes, w_scales = quantise(w_woven, "w")
+        quantise_values(woven23, 2)
+        w_codes, w_scales = quantise(w_woven, "w", None)
 
         for h in range(HALVES):
             sums = ps.tile([P, PACK, HP], F32, name="sums%d" % h)
@@ -176,7 +186,7 @@ def tile_attend_pqvalues_kernel(tc, query, keys_words, keys_scales, vbook, size,
                 start=True,
                 stop=True,
             )
-            result = sb.tile([P, E // HALVES], F32, name="result%d" % h)
+            result = tile([P, E // HALVES], F32, "result%d" % h)
             copy = (nc.vector.tensor_copy, nc.scalar.copy)[h]
             copy(result[:].rearrange("q (r j) -> q r j", j=PACK), sums[:].rearrange("q j r -> q r j"))
             queue = (nc.sync, nc.scalar)[h]

@@ -19,8 +19,12 @@ AXIS = mybir.AxisListType
 
 P = 128
 PACK = 4
+PAIR = 2
+PAIRS = PACK // PAIR
+GROUP = 16
+QUADRANT = 32
 HALVES = 2
-HP = P // HALVES
+HALF_P = P // HALVES
 
 
 def tile_attend_pqvalues_kernel(tc, query, keys_words, keys_scales, vbook, size, vsc, offs, offs2, out):
@@ -29,17 +33,16 @@ def tile_attend_pqvalues_kernel(tc, query, keys_words, keys_scales, vbook, size,
         sb = ctx.enter_context(tc.tile_pool(name="sb", bufs=1))
         ps = ctx.enter_context(tc.psum_pool(name="ps", bufs=1))
 
-        def tile(shape, dtype, name, slot=None):
-            return sb.tile(shape, dtype, name=name, tag=slot or name, align_bytes=64)
+        def tile(shape, dtype, name, reuse=None):
+            return sb.tile(shape, dtype, name=name, tag=reuse or name, align_bytes=64)
 
-        key_list = sb.tile([P, I // 16], U16, name="key_list")
-        code_lists = sb.tile([P, I // 16], U16, name="code_lists")
+        key_list = sb.tile([P, I // GROUP], U16, name="key_list")
+        code_lists = sb.tile([P, I // GROUP], U16, name="code_lists")
         vsc_col = tile([P, PACK], F32, "vsc_col")
         key_words = tile([P, T], I32, "key_words")
         key_bytes = tile([P, T], U8, "key_bytes")
         q_raw = tile([P, PACK, Q], F32, "q_raw")
         ident = tile([P, P], F32, "ident")
-        warm_out = tile([P, 1], F32, "warm_out")
 
         nc.vector.memset(key_bytes[:].bitcast(I32), 0)
         make_identity(nc, ident[:])
@@ -47,20 +50,19 @@ def tile_attend_pqvalues_kernel(tc, query, keys_words, keys_scales, vbook, size,
         book_rows = vbook.rearrange("(p j) c -> j p c", j=PACK)
         books = []
 
-        def load_book(j, slot):
-            book = tile([P, C], F32, "book%d" % j, slot)
+        def load_book(j, reuse):
+            book = tile([P, C], F32, "book%d" % j, reuse)
             nc.sync.dma_start(book[:], book_rows[j])
             books.append(book)
 
         nc.scalar.dma_start(vsc_col[:], vsc.rearrange("(p t) o -> p (t o)", t=PACK))
         size_col = tile([P, PACK], F32, "size_col")
         nc.scalar.dma_start(size_col[:], size.rearrange("o (p t) -> p (o t)", t=PACK))
-        for quad in range(4):
+        for quad in range(P // QUADRANT):
             nc.scalar.dma_start(
-                key_bytes[32 * quad : 32 * quad + 4, :].bitcast(I32),
-                keys_scales[0, 4 * quad : 4 * quad + 4, :].bitcast(I32),
+                key_bytes[QUADRANT * quad : QUADRANT * quad + PACK, :].bitcast(I32),
+                keys_scales[0, PACK * quad : PACK * quad + PACK, :].bitcast(I32),
             )
-        nc.scalar.activation(warm_out[:], ident[:, 0:1], ACT.Exp)
         nc.sync.dma_start(code_lists[:], offs2)
         nc.sync.dma_start(key_list[:], offs)
         load_book(0, None)
@@ -79,50 +81,49 @@ def tile_attend_pqvalues_kernel(tc, query, keys_words, keys_scales, vbook, size,
         nc.vector.tensor_copy(
             vsc_row[:].rearrange("p (n t) -> p n t", t=PACK), vsc_bank[:].rearrange("p t n -> p n t")
         )
-        load_book(2, "vsc_col")
 
-
-        def values(j, slot):
-            prod = tile([P, I], F32, "prod%d" % j, slot)
+        def values(j, reuse):
+            prod = tile([P, I], F32, "prod%d" % j, reuse)
             nc.vector.tensor_tensor(prod[:], books[j][:].indirect(code_lists[:]), vsc_row[:], ALU.mult)
-            rounded = tile([P, 2, P, 2], BF16, "rounded%d" % j)
-            nc.scalar.copy(rounded[:], prod[:].rearrange("p (n u e) -> p u n e", u=2, e=2))
-            bank = ps.tile([P, 2, P], F32, name="v%d_bank" % j, tag="vbank%d" % (j % 2))
-            for u in range(2):
-                words = rounded[:, u].rearrange("p n e -> p (n e)").bitcast(F32)
+            rounded = tile([P, PAIRS, P, PAIR], BF16, "rounded%d" % j)
+            nc.scalar.copy(rounded[:], prod[:].rearrange("p (n u s) -> p u n s", u=PAIRS, s=PAIR))
+            bank = ps.tile([P, PAIRS, P], F32, name="v%d_bank" % j, tag="v_bank%d" % (j % 2))
+            for u in range(PAIRS):
+                words = rounded[:, u].rearrange("p n s -> p (n s)").bitcast(F32)
                 nc.tensor.transpose(bank[:, u, :], words, ident[:])
             return bank
 
         def weave_values(woven, j, bank):
             nc.scalar.copy(
-                woven[:, :, j % 2, :].bitcast(F32).rearrange("p h (r u) -> p h r u", u=2),
-                bank[:].rearrange("p u (h r) -> p h r u", h=HALVES),
+                woven[:, :, j % 2, :].bitcast(F32).rearrange("n h (r u) -> n h r u", u=PAIRS),
+                bank[:].rearrange("n u (h r) -> n h r u", h=HALVES),
             )
 
         def quantise_values(woven, first):
-            last = first + 2
             for h in range(HALVES):
                 nc.vector.quantize_mx(
-                    out=v_codes[:, h, first:last, :].rearrange("p j r -> p (j r)").bitcast(FP8X4),
-                    scales=v_scales[:, h, first:last, :].rearrange("p j r -> p (j r)"),
-                    in_=woven[:, h, :, :].rearrange("p j r -> p (j r)"),
+                    out=v_codes[:, h, first : first + 2, :].rearrange("n j r -> n (j r)").bitcast(FP8X4),
+                    scales=v_scales[:, h, first : first + 2, :].rearrange("n j r -> n (j r)"),
+                    in_=woven[:, h, :, :].rearrange("n j r -> n (j r)"),
                 )
 
-        def quantise(woven, name, slot):
-            codes = tile([P, P], U32, name + "_codes", slot)
-            scales = tile([P, P], U8, name + "_scales")
+        def quantise_stationary(woven, name, reuse):
+            codes = tile([P, Q], U32, name + "_codes", reuse)
+            scales = tile([P, Q], U8, name + "_scales")
             nc.vector.quantize_mx(out=codes[:].bitcast(FP8X4), scales=scales[:], in_=woven[:])
             return codes, scales
 
         q_woven = tile([P, Q * PACK], BF16, "q_woven")
         nc.scalar.copy(q_woven[:].rearrange("p (q j) -> p q j", j=PACK), q_raw[:].rearrange("p j q -> p q j"))
-        load_book(3, "q_raw")
-        woven01 = tile([P, HALVES, 2, HP * PACK], BF16, "woven01")
+        load_book(2, "q_raw")
+
+        woven01 = tile([P, HALVES, 2, HALF_P * PACK], BF16, "woven01")
         weave_values(woven01, 0, values(0, None))
+        load_book(3, "prod0")
         bank1 = values(1, None)
         picked_bytes = tile([P, I], U8, "picked_bytes", "book0")
         nc.vector.tensor_copy(picked_bytes[:], key_bytes[:].indirect(key_list[:]))
-        q_codes, q_scales = quantise(q_woven, "q", "book1")
+        q_codes, q_scales = quantise_stationary(q_woven, "q", "book1")
         weave_values(woven01, 1, bank1)
 
         picked_words = tile([P, I], U32, "picked_words", "key_bytes")
@@ -146,43 +147,44 @@ def tile_attend_pqvalues_kernel(tc, query, keys_words, keys_scales, vbook, size,
         row_sum = tile([P, 1], F32, "row_sum")
         nc.scalar.activation(probs[:], scores[:], ACT.Exp, bias=neg_max[:], accum_out=row_sum[:])
 
-        woven23 = tile([P, HALVES, 2, HP * PACK], BF16, "woven23", "neg_max")
-        weave_values(woven23, 2, bank2)
+        woven23 = tile([P, HALVES, 2, HALF_P * PACK], BF16, "woven23", "neg_max")
         bank3 = values(3, "key_bytes")
+        weave_values(woven23, 2, bank2)
 
-        inv_sum = tile([P, 1], F32, "inv_sum", "q_raw")
+        inv_sum = tile([P, 1], F32, "inv_sum", "prod0")
         nc.vector.reciprocal(inv_sum[:], row_sum[:])
-        w_bank = ps.tile([P, 2, P], F32, name="w_bank", tag="vsc_bank")
-        for u in range(2):
-            weights = tile([P, P, 2], BF16, "weights%d" % u)
+        w_bank = ps.tile([P, PAIRS, Q], F32, name="w_bank", tag="vsc_bank")
+        for u in range(PAIRS):
+            weights = tile([P, P, PAIR], BF16, "weights%d" % u)
             nc.vector.scalar_tensor_tensor(
                 weights[:],
-                probs[:].rearrange("p (n u e) -> p u n e", u=2, e=2)[:, u],
+                probs[:].rearrange("q (n u s) -> q u n s", u=PAIRS, s=PAIR)[:, u],
                 inv_sum[:],
-                size_bank[:, 2 * u : 2 * u + 2, :].rearrange("p e n -> p n e"),
+                size_bank[:, PAIR * u : PAIR * (u + 1), :].rearrange("q s n -> q n s"),
                 ALU.mult,
                 ALU.mult,
             )
-            nc.tensor.transpose(w_bank[:, u, :], weights[:].rearrange("p n e -> p (n e)").bitcast(F32), ident[:])
+            nc.tensor.transpose(w_bank[:, u, :], weights[:].rearrange("q n s -> q (n s)").bitcast(F32), ident[:])
         weave_values(woven23, 3, bank3)
-        v_codes = tile([P, HALVES, PACK, HP], U32, "v_codes", "probs")
-        v_scales = tile([P, HALVES, PACK, HP], U8, "v_scales")
+
+        v_codes = tile([P, HALVES, PACK, HALF_P], U32, "v_codes", "probs")
+        v_scales = tile([P, HALVES, PACK, HALF_P], U8, "v_scales")
         quantise_values(woven01, 0)
         w_woven = tile([P, Q * PACK], BF16, "w_woven")
         nc.scalar.copy(
-            w_woven[:].bitcast(F32).rearrange("p (r u) -> p r u", u=2), w_bank[:].rearrange("p u r -> p r u")
+            w_woven[:].bitcast(F32).rearrange("n (q u) -> n q u", u=PAIRS), w_bank[:].rearrange("n u q -> n q u")
         )
         quantise_values(woven23, 2)
-        w_codes, w_scales = quantise(w_woven, "w", None)
+        w_codes, w_scales = quantise_stationary(w_woven, "w", None)
 
         for h in range(HALVES):
-            sums = ps.tile([P, PACK, HP], F32, name="sums%d" % h)
+            sums = ps.tile([P, PACK, HALF_P], F32, name="sums%d" % h)
             nc.tensor.matmul_mx(
                 out=sums[:].rearrange("q j r -> q (j r)"),
                 lhsT=w_codes[:].bitcast(FP8X4),
                 lhsT_scale=w_scales[:],
-                rhs=v_codes[:, h, :, :].rearrange("p j r -> p (j r)").bitcast(FP8X4),
-                rhs_scale=v_scales[:, h, :, :].rearrange("p j r -> p (j r)"),
+                rhs=v_codes[:, h, :, :].rearrange("n j r -> n (j r)").bitcast(FP8X4),
+                rhs_scale=v_scales[:, h, :, :].rearrange("n j r -> n (j r)"),
                 start=True,
                 stop=True,
             )

@@ -1,7 +1,6 @@
 from contextlib import ExitStack
 
 import concourse.mybir as mybir
-from concourse.masks import make_identity
 
 D, T, I, C, Q, E = 512, 2048, 512, 1024, 128, 512
 FLOPS = 2 * Q * I * D + 2 * Q * I * E
@@ -24,6 +23,8 @@ PAIRS = PACK // PAIR
 GROUP = 16
 QUADRANT = 32
 HALVES = 2
+EARLY = 256
+LEAD = 128
 HALF_P = P // HALVES
 
 
@@ -31,63 +32,85 @@ def tile_attend_pqvalues_kernel(tc, query, keys_words, keys_scales, vbook, size,
     nc = tc.nc
     with ExitStack() as ctx:
         sb = ctx.enter_context(tc.tile_pool(name="sb", bufs=1))
+        placed = ctx.enter_context(tc.tile_pool(name="placed", bufs=1))
         ps = ctx.enter_context(tc.psum_pool(name="ps", bufs=1))
 
         def tile(shape, dtype, name, reuse=None):
             return sb.tile(shape, dtype, name=name, tag=reuse or name, align_bytes=64)
 
+        def place(shape, dtype, name, offset):
+            return placed.tile(shape, dtype, name=name, offset=offset, align_bytes=64)
+
         key_list = sb.tile([P, I // GROUP], U16, name="key_list")
         code_lists = sb.tile([P, I // GROUP], U16, name="code_lists")
-        vsc_col = tile([P, PACK], F32, "vsc_col")
-        key_words = tile([P, T], I32, "key_words")
+        vsc_wide = place([P, 32], F32, "vsc_wide", 16384)
+        vsc_col = vsc_wide[:, 0:PACK]
         key_bytes = tile([P, T], U8, "key_bytes")
-        q_raw = tile([P, PACK, Q], F32, "q_raw")
         ident = tile([P, P], F32, "ident")
 
         nc.vector.memset(key_bytes[:].bitcast(I32), 0)
-        make_identity(nc, ident[:])
+        zeros_wide = place([P, P], F32, "zeros_wide", 8000)
+        zeros = zeros_wide[:, 0:P]
+        nc.gpsimd.memset(zeros, 0.0)
+        nc.gpsimd.affine_select(
+            out=ident[:],
+            in_=zeros,
+            compare_op=ALU.not_equal,
+            fill=1.0,
+            base=0,
+            pattern=[[-1, P]],
+            channel_multiplier=1,
+        )
 
         book_rows = vbook.rearrange("(p j) c -> j p c", j=PACK)
         books = []
 
-        def load_book(j, reuse):
-            book = tile([P, C], F32, "book%d" % j, reuse)
+        def load_book(j, offset):
+            name = "book%d" % j
+            book = tile([P, C], F32, name) if offset is None else place([P, C], F32, name, offset)
             nc.sync.dma_start(book[:], book_rows[j])
             books.append(book)
 
-        nc.scalar.dma_start(vsc_col[:], vsc.rearrange("(p t) o -> p (t o)", t=PACK))
-        size_col = tile([P, PACK], F32, "size_col")
-        nc.scalar.dma_start(size_col[:], size.rearrange("o (p t) -> p (o t)", t=PACK))
+        nc.scalar.dma_start(vsc_col, vsc.rearrange("(p t) o -> p (t o)", t=PACK))
+        nc.sync.dma_start(code_lists[:], offs2)
+        load_book(0, None)
+        nc.sync.dma_start(key_list[:], offs)
+        load_book(1, None)
         for quad in range(P // QUADRANT):
-            nc.scalar.dma_start(
+            nc.sync.dma_start(
                 key_bytes[QUADRANT * quad : QUADRANT * quad + PACK, :].bitcast(I32),
                 keys_scales[0, PACK * quad : PACK * quad + PACK, :].bitcast(I32),
             )
-        nc.sync.dma_start(code_lists[:], offs2)
-        nc.sync.dma_start(key_list[:], offs)
-        load_book(0, None)
-        load_book(1, None)
-        nc.sync.dma_start(q_raw[:], query.rearrange("(p j) q -> p j q", j=PACK))
+        key_words = place([P, T], I32, "key_words", 0)
         nc.sync.dma_start(key_words[:], keys_words[0].rearrange("p n t -> p (n t)").bitcast(I32))
+        q_raw = place([P, PACK, Q], F32, "q_raw", 8256)
+        nc.sync.dma_start(q_raw[:], query.rearrange("(p j) q -> p j q", j=PACK))
+        size_col = place([P, PACK], F32, "size_col", 8192)
+        nc.sync.dma_start(size_col[:], size.rearrange("o (p t) -> p (o t)", t=PACK))
 
-        def spread(col, name):
-            bank = ps.tile([P, PACK, P], F32, name=name)
+        def spread(col, name, tag):
+            bank = ps.tile([P, PACK, P], F32, name=name, tag=tag)
             for t in range(PACK):
                 nc.tensor.transpose(bank[:, t, :], col[:, t : t + 1].to_broadcast([P, P]), ident[:])
             return bank
 
-        vsc_bank = spread(vsc_col, "vsc_bank")
+        vsc_bank = spread(vsc_col, "vsc_bank", "vsc_bank")
         vsc_row = tile([P, I], F32, "vsc_row")
-        nc.vector.tensor_copy(
-            vsc_row[:].rearrange("p (n t) -> p n t", t=PACK), vsc_bank[:].rearrange("p t n -> p n t")
-        )
+        nc.scalar.copy(vsc_row[:].rearrange("p (n t) -> p n t", t=PACK), vsc_bank[:].rearrange("p t n -> p n t"))
+        load_book(2, 12352)
+        load_book(3, 16448)
 
-        def values(j, reuse):
-            prod = tile([P, I], F32, "prod%d" % j, reuse)
-            nc.vector.tensor_tensor(prod[:], books[j][:].indirect(code_lists[:]), vsc_row[:], ALU.mult)
-            rounded = tile([P, PAIRS, P, PAIR], BF16, "rounded%d" % j)
-            nc.scalar.copy(rounded[:], prod[:].rearrange("p (n u s) -> p u n s", u=PAIRS, s=PAIR))
-            bank = ps.tile([P, PAIRS, P], F32, name="v%d_bank" % j, tag="v_bank%d" % (j % 2))
+        def gather(j, prod, first):
+            count = prod.shape[1]
+            lists = code_lists[:, first // GROUP : (first + count) // GROUP]
+            nc.vector.tensor_tensor(prod, books[j][:].indirect(lists), vsc_row[:, first : first + count], ALU.mult)
+
+        def round_once(rounded, prod, first):
+            rows = slice(first // PACK, (first + prod.shape[1]) // PACK)
+            nc.scalar.copy(rounded[:, :, rows, :], prod.rearrange("p (n u s) -> p u n s", u=PAIRS, s=PAIR))
+
+        def turn(j, rounded):
+            bank = ps.tile([P, PAIRS, P], F32, name="v%d_bank" % j, tag="v_bank%d" % (0, 1, 0, 3)[j])
             for u in range(PAIRS):
                 words = rounded[:, u].rearrange("p n s -> p (n s)").bitcast(F32)
                 nc.tensor.transpose(bank[:, u, :], words, ident[:])
@@ -113,21 +136,27 @@ def tile_attend_pqvalues_kernel(tc, query, keys_words, keys_scales, vbook, size,
             nc.vector.quantize_mx(out=codes[:].bitcast(FP8X4), scales=scales[:], in_=woven[:])
             return codes, scales
 
-        q_woven = tile([P, Q * PACK], BF16, "q_woven")
-        nc.scalar.copy(q_woven[:].rearrange("p (q j) -> p q j", j=PACK), q_raw[:].rearrange("p j q -> p q j"))
-        load_book(2, "q_raw")
-
-        woven01 = tile([P, HALVES, 2, HALF_P * PACK], BF16, "woven01")
-        weave_values(woven01, 0, values(0, None))
-        load_book(3, "prod0")
-        bank1 = values(1, None)
-        picked_bytes = tile([P, I], U8, "picked_bytes", "book0")
+        pair_shape = [P, PAIRS, P, PAIR]
+        prod0 = tile([P, I], F32, "prod0")
+        gather(0, prod0[:], 0)
+        rounded0 = tile(pair_shape, BF16, "rounded0")
+        round_once(rounded0, prod0[:], 0)
+        bank0 = turn(0, rounded0)
+        rounded1 = tile(pair_shape, BF16, "rounded1")
+        for first, count, offset in ((0, LEAD, 32768), (LEAD, I - LEAD, 28672 - 512)):
+            wide = place([P, I - LEAD], F32, "prod1_%d" % first, offset)
+            gather(1, wide[:, 0:count], first)
+            round_once(rounded1, wide[:, 0:count], first)
+        woven01 = place([P, HALVES, 2, HALF_P * PACK], BF16, "woven01", 32768 + 512)
+        weave_values(woven01, 0, bank0)
+        weave_values(woven01, 1, turn(1, rounded1))
+        picked_bytes = place([P, I], U8, "picked_bytes", 32768)
         nc.vector.tensor_copy(picked_bytes[:], key_bytes[:].indirect(key_list[:]))
-        q_codes, q_scales = quantise_stationary(q_woven, "q", "book1")
-        weave_values(woven01, 1, bank1)
-
-        picked_words = tile([P, I], U32, "picked_words", "key_bytes")
+        picked_words = place([P, I], U32, "picked_words", 28672)
         nc.vector.tensor_copy(picked_words[:], key_words[:].bitcast(U32).indirect(key_list[:]))
+        q_woven = place([P, Q * PACK], BF16, "q_woven", 28672 - 1024)
+        nc.scalar.copy(q_woven[:].rearrange("p (q j) -> p q j", j=PACK), q_raw[:].rearrange("p j q -> p q j"))
+        q_codes, q_scales = quantise_stationary(q_woven, "q", None)
         scores = ps.tile([P, I], F32, name="scores")
         nc.tensor.matmul_mx(
             out=scores[:],
@@ -138,20 +167,31 @@ def tile_attend_pqvalues_kernel(tc, query, keys_words, keys_scales, vbook, size,
             start=True,
             stop=True,
         )
-        bank2 = values(2, "q_woven")
-        size_bank = spread(size_col, "size_bank")
+        size_bank = spread(size_col, "size_bank", "v_bank1")
+        rounded2 = tile(pair_shape, BF16, "rounded2")
+        for first, count, offset in ((0, LEAD, 20544), (LEAD, I - LEAD, 36864)):
+            wide = place([P, 1024], F32, "prod2_%d" % first, offset)
+            gather(2, wide[:, 0:count], first)
+            round_once(rounded2, wide[:, 0:count], first)
+        bank2 = turn(2, rounded2)
 
-        neg_max = tile([P, 1], F32, "neg_max")
-        nc.vector.tensor_reduce(neg_max[:], scores[:], AXIS.X, ALU.max, negate=True)
+        max_wide = place([P, 32], F32, "max_wide", 20544 + 1024)
+        neg_max = max_wide[:, 0:1]
+        nc.vector.tensor_reduce(neg_max, scores[:], AXIS.X, ALU.max, negate=True)
         probs = tile([P, I], F32, "probs")
         row_sum = tile([P, 1], F32, "row_sum")
-        nc.scalar.activation(probs[:], scores[:], ACT.Exp, bias=neg_max[:], accum_out=row_sum[:])
+        nc.scalar.activation(probs[:], scores[:], ACT.Exp, bias=neg_max, accum_out=row_sum[:])
 
-        woven23 = tile([P, HALVES, 2, HALF_P * PACK], BF16, "woven23", "neg_max")
-        bank3 = values(3, "key_bytes")
+        rounded3 = place(pair_shape, BF16, "rounded3", 20544 + 1024)
+        for first in (0, EARLY):
+            prod3 = place([P, EARLY], F32, "prod3_%d" % first, 20544 + 12 * first)
+            gather(3, prod3[:], first)
+            round_once(rounded3, prod3[:], first)
+        bank3 = turn(3, rounded3)
+        woven23 = place([P, HALVES, 2, HALF_P * PACK], BF16, "woven23", 20544 + 3072 + 512)
         weave_values(woven23, 2, bank2)
 
-        inv_sum = tile([P, 1], F32, "inv_sum", "prod0")
+        inv_sum = tile([P, 1], F32, "inv_sum")
         nc.vector.reciprocal(inv_sum[:], row_sum[:])
         w_bank = ps.tile([P, PAIRS, Q], F32, name="w_bank", tag="vsc_bank")
         for u in range(PAIRS):

@@ -96,7 +96,10 @@ def tile_attend_pqvalues_kernel(tc, query, keys_words, keys_scales, vbook, size,
 
         vsc_bank = spread(vsc_col, "vsc_bank", "vsc_bank")
         vsc_row = tile([P, I], F32, "vsc_row")
-        nc.scalar.copy(vsc_row[:].rearrange("p (n t) -> p n t", t=PACK), vsc_bank[:].rearrange("p t n -> p n t"))
+        for rows in (slice(0, LEAD // PACK), slice(LEAD // PACK, P)):
+            nc.scalar.copy(
+                vsc_row[:].rearrange("p (n t) -> p n t", t=PACK)[:, rows], vsc_bank[:].rearrange("p t n -> p n t")[:, rows]
+            )
         load_book(2, 12352)
         load_book(3, 16448)
 
@@ -138,12 +141,13 @@ def tile_attend_pqvalues_kernel(tc, query, keys_words, keys_scales, vbook, size,
 
         pair_shape = [P, PAIRS, P, PAIR]
         prod0 = tile([P, I], F32, "prod0")
-        gather(0, prod0[:], 0)
+        gather(0, prod0[:, 0:LEAD], 0)
+        gather(0, prod0[:, LEAD:I], LEAD)
         rounded0 = tile(pair_shape, BF16, "rounded0")
         round_once(rounded0, prod0[:], 0)
         bank0 = turn(0, rounded0)
         rounded1 = tile(pair_shape, BF16, "rounded1")
-        for first, count, offset in ((0, LEAD, 32768), (LEAD, I - LEAD, 28672 - 512)):
+        for first, count, offset in ((I - LEAD, LEAD, 32768), (0, I - LEAD, 28672 - 512)):
             wide = place([P, I - LEAD], F32, "prod1_%d" % first, offset)
             gather(1, wide[:, 0:count], first)
             round_once(rounded1, wide[:, 0:count], first)
@@ -178,15 +182,16 @@ def tile_attend_pqvalues_kernel(tc, query, keys_words, keys_scales, vbook, size,
         max_wide = place([P, 32], F32, "max_wide", 20544 + 1024)
         neg_max = max_wide[:, 0:1]
         nc.vector.tensor_reduce(neg_max, scores[:], AXIS.X, ALU.max, negate=True)
-        probs = tile([P, I], F32, "probs")
+        probs = tile([P, PAIRS, P, PAIR], F32, "probs")
         row_sum = tile([P, 1], F32, "row_sum")
-        nc.scalar.activation(probs[:], scores[:], ACT.Exp, bias=neg_max, accum_out=row_sum[:])
+        scores_by_pair = scores[:].rearrange("q (n u s) -> q u n s", u=PAIRS, s=PAIR)
+        nc.scalar.activation(probs[:], scores_by_pair, ACT.Exp, bias=neg_max, accum_out=row_sum[:])
 
         rounded3 = place(pair_shape, BF16, "rounded3", 20544 + 1024)
-        for first in (0, EARLY):
-            prod3 = place([P, EARLY], F32, "prod3_%d" % first, 20544 + 12 * first)
-            gather(3, prod3[:], first)
-            round_once(rounded3, prod3[:], first)
+        for first, count, offset in ((0, 256, 20544), (256, 128, 20544 + 2048), (384, 128, 20544 + 3072)):
+            prod3 = place([P, 256], F32, "prod3_%d" % first, offset)
+            gather(3, prod3[:, 0:count], first)
+            round_once(rounded3, prod3[:, 0:count], first)
         bank3 = turn(3, rounded3)
         woven23 = place([P, HALVES, 2, HALF_P * PACK], BF16, "woven23", 20544 + 3072 + 512)
         weave_values(woven23, 2, bank2)
@@ -198,7 +203,7 @@ def tile_attend_pqvalues_kernel(tc, query, keys_words, keys_scales, vbook, size,
             weights = tile([P, P, PAIR], BF16, "weights%d" % u)
             nc.vector.scalar_tensor_tensor(
                 weights[:],
-                probs[:].rearrange("q (n u s) -> q u n s", u=PAIRS, s=PAIR)[:, u],
+                probs[:, u],
                 inv_sum[:],
                 size_bank[:, PAIR * u : PAIR * (u + 1), :].rearrange("q s n -> q n s"),
                 ALU.mult,

@@ -23,9 +23,12 @@ PAIRS = PACK // PAIR
 GROUP = 16
 QUADRANT = 32
 HALVES = 2
-EARLY = 256
-LEAD = 128
 HALF_P = P // HALVES
+SHORT = 128
+LONG = I - SHORT
+KIB = 1024
+STRETCH = 8 * KIB
+IDENTITY, VSC_TURNED, SHORT1_ROUNDED, BOOK0_TURNED, SHORT2_ROUNDED = 0, 2, 3, 4, 5
 
 
 def tile_attend_pqvalues_kernel(tc, query, keys_words, keys_scales, vbook, size, vsc, offs, offs2, out):
@@ -35,22 +38,23 @@ def tile_attend_pqvalues_kernel(tc, query, keys_words, keys_scales, vbook, size,
         placed = ctx.enter_context(tc.tile_pool(name="placed", bufs=1))
         ps = ctx.enter_context(tc.psum_pool(name="ps", bufs=1))
 
-        def tile(shape, dtype, name, reuse=None):
-            return sb.tile(shape, dtype, name=name, tag=reuse or name, align_bytes=64)
+        def tile(shape, dtype, name, tag=None):
+            return sb.tile(shape, dtype, name=name, tag=tag or name, align_bytes=64)
 
-        def place(shape, dtype, name, offset):
-            return placed.tile(shape, dtype, name=name, offset=offset, align_bytes=64)
+        def place(shape, dtype, name, stretch, kib=0):
+            return placed.tile(shape, dtype, name=name, offset=stretch * STRETCH + kib * KIB, align_bytes=64)
+
+        def first_tenant(columns, name, stretch, stretches=1):
+            return place([P, stretches * STRETCH // 4], F32, name, stretch)[:, 0:columns]
 
         key_list = sb.tile([P, I // GROUP], U16, name="key_list")
         code_lists = sb.tile([P, I // GROUP], U16, name="code_lists")
-        vsc_wide = place([P, 32], F32, "vsc_wide", 16384)
-        vsc_col = vsc_wide[:, 0:PACK]
+        vsc_col = first_tenant(PACK, "vsc_col", VSC_TURNED)
         key_bytes = tile([P, T], U8, "key_bytes")
         ident = tile([P, P], F32, "ident")
 
         nc.vector.memset(key_bytes[:].bitcast(I32), 0)
-        zeros_wide = place([P, P], F32, "zeros_wide", 8000)
-        zeros = zeros_wide[:, 0:P]
+        zeros = first_tenant(P, "zeros", IDENTITY, 2)
         nc.gpsimd.memset(zeros, 0.0)
         nc.gpsimd.affine_select(
             out=ident[:],
@@ -65,27 +69,25 @@ def tile_attend_pqvalues_kernel(tc, query, keys_words, keys_scales, vbook, size,
         book_rows = vbook.rearrange("(p j) c -> j p c", j=PACK)
         books = []
 
-        def load_book(j, offset):
-            name = "book%d" % j
-            book = tile([P, C], F32, name) if offset is None else place([P, C], F32, name, offset)
-            nc.sync.dma_start(book[:], book_rows[j])
+        def load_book(book):
+            nc.sync.dma_start(book[:], book_rows[len(books)])
             books.append(book)
 
         nc.scalar.dma_start(vsc_col, vsc.rearrange("(p t) o -> p (t o)", t=PACK))
         nc.sync.dma_start(code_lists[:], offs2)
-        load_book(0, None)
+        load_book(tile([P, C], F32, "book0"))
         nc.sync.dma_start(key_list[:], offs)
-        load_book(1, None)
+        load_book(tile([P, C], F32, "book1"))
         for quad in range(P // QUADRANT):
             nc.sync.dma_start(
                 key_bytes[QUADRANT * quad : QUADRANT * quad + PACK, :].bitcast(I32),
                 keys_scales[0, PACK * quad : PACK * quad + PACK, :].bitcast(I32),
             )
-        key_words = place([P, T], I32, "key_words", 0)
+        key_words = place([P, T], I32, "key_words", IDENTITY)
         nc.sync.dma_start(key_words[:], keys_words[0].rearrange("p n t -> p (n t)").bitcast(I32))
-        q_raw = place([P, PACK, Q], F32, "q_raw", 8256)
+        q_raw = place([P, PACK, Q], F32, "q_raw", IDENTITY + 1)
         nc.sync.dma_start(q_raw[:], query.rearrange("(p j) q -> p j q", j=PACK))
-        size_col = place([P, PACK], F32, "size_col", 8192)
+        size_col = place([P, PACK], F32, "size_col", IDENTITY + 1, 2)
         nc.sync.dma_start(size_col[:], size.rearrange("o (p t) -> p (o t)", t=PACK))
 
         def spread(col, name, tag):
@@ -94,26 +96,25 @@ def tile_attend_pqvalues_kernel(tc, query, keys_words, keys_scales, vbook, size,
                 nc.tensor.transpose(bank[:, t, :], col[:, t : t + 1].to_broadcast([P, P]), ident[:])
             return bank
 
-        vsc_bank = spread(vsc_col, "vsc_bank", "vsc_bank")
+        vsc_bank = spread(vsc_col, "vsc_bank", "bank_a")
         vsc_row = tile([P, I], F32, "vsc_row")
-        for rows in (slice(0, LEAD // PACK), slice(LEAD // PACK, P)):
+        for rows in (slice(0, SHORT // PACK), slice(SHORT // PACK, P)):
             nc.scalar.copy(
-                vsc_row[:].rearrange("p (n t) -> p n t", t=PACK)[:, rows], vsc_bank[:].rearrange("p t n -> p n t")[:, rows]
+                vsc_row[:].rearrange("p (n t) -> p n t", t=PACK)[:, rows],
+                vsc_bank[:].rearrange("p t n -> p n t")[:, rows],
             )
-        load_book(2, 12352)
-        load_book(3, 16448)
+        load_book(place([P, C], F32, "book2", VSC_TURNED))
+        load_book(place([P, C], F32, "book3", VSC_TURNED, 4))
 
-        def gather(j, prod, first):
+        def gather_and_round(j, prod, first, rounded):
             count = prod.shape[1]
             lists = code_lists[:, first // GROUP : (first + count) // GROUP]
             nc.vector.tensor_tensor(prod, books[j][:].indirect(lists), vsc_row[:, first : first + count], ALU.mult)
-
-        def round_once(rounded, prod, first):
-            rows = slice(first // PACK, (first + prod.shape[1]) // PACK)
+            rows = slice(first // PACK, (first + count) // PACK)
             nc.scalar.copy(rounded[:, :, rows, :], prod.rearrange("p (n u s) -> p u n s", u=PAIRS, s=PAIR))
 
-        def turn(j, rounded):
-            bank = ps.tile([P, PAIRS, P], F32, name="v%d_bank" % j, tag="v_bank%d" % (0, 1, 0, 3)[j])
+        def turn(rounded, name, tag):
+            bank = ps.tile([P, PAIRS, P], F32, name=name, tag=tag)
             for u in range(PAIRS):
                 words = rounded[:, u].rearrange("p n s -> p (n s)").bitcast(F32)
                 nc.tensor.transpose(bank[:, u, :], words, ident[:])
@@ -133,34 +134,34 @@ def tile_attend_pqvalues_kernel(tc, query, keys_words, keys_scales, vbook, size,
                     in_=woven[:, h, :, :].rearrange("n j r -> n (j r)"),
                 )
 
-        def quantise_stationary(woven, name, reuse):
-            codes = tile([P, Q], U32, name + "_codes", reuse)
+        def quantise_stationary(woven, name):
+            codes = tile([P, Q], U32, name + "_codes")
             scales = tile([P, Q], U8, name + "_scales")
             nc.vector.quantize_mx(out=codes[:].bitcast(FP8X4), scales=scales[:], in_=woven[:])
             return codes, scales
 
         pair_shape = [P, PAIRS, P, PAIR]
-        prod0 = tile([P, I], F32, "prod0")
-        gather(0, prod0[:, 0:LEAD], 0)
-        gather(0, prod0[:, LEAD:I], LEAD)
-        rounded0 = tile(pair_shape, BF16, "rounded0")
-        round_once(rounded0, prod0[:], 0)
-        bank0 = turn(0, rounded0)
+        woven_shape = [P, HALVES, 2, HALF_P * PACK]
+
+        rounded0_words = first_tenant(I // PAIR, "rounded0", BOOK0_TURNED)
+        rounded0 = rounded0_words.bitcast(BF16).rearrange("p (u n s) -> p u n s", u=PAIRS, s=PAIR)
+        gather_and_round(0, tile([P, SHORT], F32, "short0")[:], 0, rounded0)
+        gather_and_round(0, tile([P, LONG], F32, "long0")[:], SHORT, rounded0)
+        bank0 = turn(rounded0, "v0_bank", "bank_b")
         rounded1 = tile(pair_shape, BF16, "rounded1")
-        for first, count, offset in ((I - LEAD, LEAD, 32768), (0, I - LEAD, 28672 - 512)):
-            wide = place([P, I - LEAD], F32, "prod1_%d" % first, offset)
-            gather(1, wide[:, 0:count], first)
-            round_once(rounded1, wide[:, 0:count], first)
-        woven01 = place([P, HALVES, 2, HALF_P * PACK], BF16, "woven01", 32768 + 512)
+        gather_and_round(1, first_tenant(SHORT, "short1", SHORT1_ROUNDED), LONG, rounded1)
+        gather_and_round(1, tile([P, LONG], F32, "long1")[:], 0, rounded1)
+        woven01 = place(woven_shape, BF16, "woven01", SHORT1_ROUNDED, 2)
         weave_values(woven01, 0, bank0)
-        weave_values(woven01, 1, turn(1, rounded1))
-        picked_bytes = place([P, I], U8, "picked_bytes", 32768)
+        weave_values(woven01, 1, turn(rounded1, "v1_bank", "bank_c"))
+
+        picked_bytes = place([P, I], U8, "picked_bytes", SHORT1_ROUNDED)
         nc.vector.tensor_copy(picked_bytes[:], key_bytes[:].indirect(key_list[:]))
-        picked_words = place([P, I], U32, "picked_words", 28672)
+        picked_words = place([P, I], U32, "picked_words", BOOK0_TURNED)
         nc.vector.tensor_copy(picked_words[:], key_words[:].bitcast(U32).indirect(key_list[:]))
-        q_woven = place([P, Q * PACK], BF16, "q_woven", 28672 - 1024)
+        q_woven = place([P, Q * PACK], BF16, "q_woven", BOOK0_TURNED, 2)
         nc.scalar.copy(q_woven[:].rearrange("p (q j) -> p q j", j=PACK), q_raw[:].rearrange("p j q -> p q j"))
-        q_codes, q_scales = quantise_stationary(q_woven, "q", None)
+        q_codes, q_scales = quantise_stationary(q_woven, "q")
         scores = ps.tile([P, I], F32, name="scores")
         nc.tensor.matmul_mx(
             out=scores[:],
@@ -171,34 +172,31 @@ def tile_attend_pqvalues_kernel(tc, query, keys_words, keys_scales, vbook, size,
             start=True,
             stop=True,
         )
-        size_bank = spread(size_col, "size_bank", "v_bank1")
-        rounded2 = tile(pair_shape, BF16, "rounded2")
-        for first, count, offset in ((0, LEAD, 20544), (LEAD, I - LEAD, 36864)):
-            wide = place([P, 1024], F32, "prod2_%d" % first, offset)
-            gather(2, wide[:, 0:count], first)
-            round_once(rounded2, wide[:, 0:count], first)
-        bank2 = turn(2, rounded2)
+        size_bank = spread(size_col, "size_bank", "bank_c")
 
-        max_wide = place([P, 32], F32, "max_wide", 20544 + 1024)
-        neg_max = max_wide[:, 0:1]
-        nc.vector.tensor_reduce(neg_max, scores[:], AXIS.X, ALU.max, negate=True)
-        probs = tile([P, PAIRS, P, PAIR], F32, "probs")
+        rounded2 = tile(pair_shape, BF16, "rounded2")
+        gather_and_round(2, first_tenant(SHORT, "short2", SHORT2_ROUNDED), 0, rounded2)
+        gather_and_round(2, tile([P, LONG], F32, "long2")[:], SHORT, rounded2)
+        bank2 = turn(rounded2, "v2_bank", "bank_b")
+
+        neg_max = place([P, 1], F32, "neg_max", SHORT2_ROUNDED, 4)
+        nc.vector.tensor_reduce(neg_max[:], scores[:], AXIS.X, ALU.max, negate=True)
+        probs = tile(pair_shape, F32, "probs")
         row_sum = tile([P, 1], F32, "row_sum")
         scores_by_pair = scores[:].rearrange("q (n u s) -> q u n s", u=PAIRS, s=PAIR)
-        nc.scalar.activation(probs[:], scores_by_pair, ACT.Exp, bias=neg_max, accum_out=row_sum[:])
+        nc.scalar.activation(probs[:], scores_by_pair, ACT.Exp, bias=neg_max[:], accum_out=row_sum[:])
 
-        rounded3 = place(pair_shape, BF16, "rounded3", 20544 + 1024)
-        for first, count, offset in ((0, 256, 20544), (256, 128, 20544 + 2048), (384, 128, 20544 + 3072)):
-            prod3 = place([P, 256], F32, "prod3_%d" % first, offset)
-            gather(3, prod3[:, 0:count], first)
-            round_once(rounded3, prod3[:, 0:count], first)
-        bank3 = turn(3, rounded3)
-        woven23 = place([P, HALVES, 2, HALF_P * PACK], BF16, "woven23", 20544 + 3072 + 512)
+        rounded3 = place(pair_shape, BF16, "rounded3", SHORT2_ROUNDED, 4)
+        for kib, (first, count) in enumerate(((0, I - 2 * SHORT), (I - 2 * SHORT, SHORT), (LONG, SHORT))):
+            piece = place([P, count], F32, "piece3_%d" % kib, SHORT2_ROUNDED, kib)
+            gather_and_round(3, piece[:], first, rounded3)
+        bank3 = turn(rounded3, "v3_bank", "bank_d")
+        woven23 = place(woven_shape, BF16, "woven23", SHORT2_ROUNDED, 2)
         weave_values(woven23, 2, bank2)
 
         inv_sum = tile([P, 1], F32, "inv_sum")
         nc.vector.reciprocal(inv_sum[:], row_sum[:])
-        w_bank = ps.tile([P, PAIRS, Q], F32, name="w_bank", tag="vsc_bank")
+        w_bank = ps.tile([P, PAIRS, Q], F32, name="w_bank", tag="bank_a")
         for u in range(PAIRS):
             weights = tile([P, P, PAIR], BF16, "weights%d" % u)
             nc.vector.scalar_tensor_tensor(
@@ -220,7 +218,7 @@ def tile_attend_pqvalues_kernel(tc, query, keys_words, keys_scales, vbook, size,
             w_woven[:].bitcast(F32).rearrange("n (q u) -> n q u", u=PAIRS), w_bank[:].rearrange("n u q -> n q u")
         )
         quantise_values(woven23, 2)
-        w_codes, w_scales = quantise_stationary(w_woven, "w", None)
+        w_codes, w_scales = quantise_stationary(w_woven, "w")
 
         for h in range(HALVES):
             sums = ps.tile([P, PACK, HALF_P], F32, name="sums%d" % h)

@@ -54,17 +54,9 @@ def tile_attend_pqvalues_kernel(tc, query, keys_words, keys_scales, vbook, size,
         ident = tile([P, P], F32, "ident")
 
         nc.vector.memset(key_bytes[:].bitcast(I32), 0)
-        zeros = first_tenant(P, "zeros", IDENTITY, 2)
-        nc.gpsimd.memset(zeros, 0.0)
-        nc.gpsimd.affine_select(
-            out=ident[:],
-            in_=zeros,
-            compare_op=ALU.not_equal,
-            fill=1.0,
-            base=0,
-            pattern=[[-1, P]],
-            channel_multiplier=1,
-        )
+        distance = first_tenant(P, "distance", IDENTITY, 2)
+        nc.gpsimd.iota(distance, [[1, P]], base=0, channel_multiplier=-1, allow_small_or_imprecise_dtypes=True)
+        nc.vector.tensor_scalar(ident[:], distance, 0.0, None, ALU.is_equal)
 
         book_rows = vbook.rearrange("(p j) c -> j p c", j=PACK)
         books = []

@@ -28,7 +28,7 @@ SHORT = 128
 LONG = I - SHORT
 KIB = 1024
 STRETCH = 8 * KIB
-IDENTITY, VSC_TURNED, SHORT1_ROUNDED, BOOK0_TURNED, SHORT2_ROUNDED = 0, 2, 3, 4, 5
+IDENTITY, SHORT2_ROUNDED, SHORT1_ROUNDED, BOOK0_TURNED, BYTES_PICKED = 0, 2, 3, 4, 5
 
 
 def tile_attend_pqvalues_kernel(tc, query, keys_words, keys_scales, vbook, size, vsc, offs, offs2, out):
@@ -49,11 +49,11 @@ def tile_attend_pqvalues_kernel(tc, query, keys_words, keys_scales, vbook, size,
 
         key_list = sb.tile([P, I // GROUP], U16, name="key_list")
         code_lists = sb.tile([P, I // GROUP], U16, name="code_lists")
-        vsc_col = first_tenant(PACK, "vsc_col", VSC_TURNED)
-        key_bytes = tile([P, T], U8, "key_bytes")
+        vsc_col = tile([P, PACK], F32, "vsc_col")[:]
+        key_bytes = place([P, 2 * STRETCH], U8, "key_bytes", BYTES_PICKED)[:, 0:T]
         ident = tile([P, P], F32, "ident")
 
-        nc.vector.memset(key_bytes[:].bitcast(I32), 0)
+        nc.vector.memset(key_bytes.bitcast(I32), 0)
         distance = first_tenant(P, "distance", IDENTITY, 2)
         nc.gpsimd.iota(distance, [[1, P]], base=0, channel_multiplier=-1, allow_small_or_imprecise_dtypes=True)
         nc.vector.tensor_scalar(ident[:], distance, 0.0, None, ALU.is_equal)
@@ -66,21 +66,17 @@ def tile_attend_pqvalues_kernel(tc, query, keys_words, keys_scales, vbook, size,
             books.append(book)
 
         nc.scalar.dma_start(vsc_col, vsc.rearrange("(p t) o -> p (t o)", t=PACK))
-        nc.sync.dma_start(code_lists[:], offs2)
-        load_book(tile([P, C], F32, "book0"))
         nc.sync.dma_start(key_list[:], offs)
-        load_book(tile([P, C], F32, "book1"))
-        for quad in range(P // QUADRANT):
-            nc.sync.dma_start(
-                key_bytes[QUADRANT * quad : QUADRANT * quad + PACK, :].bitcast(I32),
-                keys_scales[0, PACK * quad : PACK * quad + PACK, :].bitcast(I32),
-            )
+        load_book(tile([P, C], F32, "book0"))
+        nc.sync.dma_start(code_lists[:], offs2)
+        nc.sync.dma_start(key_bytes[0:P:8, :].bitcast(I32), keys_scales[0].bitcast(I32))
+        load_book(place([P, C], F32, "book1", IDENTITY + 1))
+        q_raw = place([P, PACK, Q], F32, "q_raw", IDENTITY + 1, 6)
+        nc.sync.dma_start(q_raw[:], query.rearrange("(p j) q -> p j q", j=PACK))
         key_words = place([P, T], I32, "key_words", IDENTITY)
         nc.sync.dma_start(key_words[:], keys_words[0].rearrange("p n t -> p (n t)").bitcast(I32))
-        q_raw = place([P, PACK, Q], F32, "q_raw", IDENTITY + 1)
-        nc.sync.dma_start(q_raw[:], query.rearrange("(p j) q -> p j q", j=PACK))
-        size_col = place([P, PACK], F32, "size_col", IDENTITY + 1, 2)
-        nc.sync.dma_start(size_col[:], size.rearrange("o (p t) -> p (o t)", t=PACK))
+        picked_bytes = place([P, I], U8, "picked_bytes", IDENTITY + 1, 4)
+        nc.vector.tensor_copy(picked_bytes[:], key_bytes.indirect(key_list[:]))
 
         def spread(col, name, tag):
             bank = ps.tile([P, PACK, P], F32, name=name, tag=tag)
@@ -90,13 +86,18 @@ def tile_attend_pqvalues_kernel(tc, query, keys_words, keys_scales, vbook, size,
 
         vsc_bank = spread(vsc_col, "vsc_bank", "bank_a")
         vsc_row = tile([P, I], F32, "vsc_row")
-        for rows in (slice(0, SHORT // PACK), slice(SHORT // PACK, P)):
-            nc.scalar.copy(
-                vsc_row[:].rearrange("p (n t) -> p n t", t=PACK)[:, rows],
-                vsc_bank[:].rearrange("p t n -> p n t")[:, rows],
+        nc.scalar.copy(vsc_row[:].rearrange("p (n t) -> p n t", t=PACK), vsc_bank[:].rearrange("p t n -> p n t"))
+        key_scales = tile([P, I], U8, "key_scales")
+        nc.vector.memset(key_scales[:].bitcast(I32), 0)
+        for quad in range(P // QUADRANT):
+            nc.sync.dma_start(
+                key_scales[QUADRANT * quad : QUADRANT * quad + PACK, :].bitcast(I32),
+                picked_bytes[QUADRANT * quad : QUADRANT * (quad + 1) : 8, :].bitcast(I32),
             )
-        load_book(place([P, C], F32, "book2", VSC_TURNED))
-        load_book(place([P, C], F32, "book3", VSC_TURNED, 4))
+        size_col = place([P, PACK], F32, "size_col", BYTES_PICKED)
+        nc.sync.dma_start(size_col[:], size.rearrange("o (p t) -> p (o t)", t=PACK))
+        load_book(place([P, C], F32, "book2", BYTES_PICKED, 1))
+        load_book(place([P, C], F32, "book3", BYTES_PICKED, 5))
 
         def gather_and_round(j, prod, first, rounded):
             count = prod.shape[1]
@@ -126,8 +127,7 @@ def tile_attend_pqvalues_kernel(tc, query, keys_words, keys_scales, vbook, size,
                     in_=woven[:, h, :, :].rearrange("n j r -> n (j r)"),
                 )
 
-        def quantise_stationary(woven, name):
-            codes = tile([P, Q], U32, name + "_codes")
+        def quantise_stationary(woven, name, codes):
             scales = tile([P, Q], U8, name + "_scales")
             nc.vector.quantize_mx(out=codes[:].bitcast(FP8X4), scales=scales[:], in_=woven[:])
             return codes, scales
@@ -135,41 +135,35 @@ def tile_attend_pqvalues_kernel(tc, query, keys_words, keys_scales, vbook, size,
         pair_shape = [P, PAIRS, P, PAIR]
         woven_shape = [P, HALVES, 2, HALF_P * PACK]
 
-        rounded0_words = first_tenant(I // PAIR, "rounded0", BOOK0_TURNED)
-        rounded0 = rounded0_words.bitcast(BF16).rearrange("p (u n s) -> p u n s", u=PAIRS, s=PAIR)
-        gather_and_round(0, tile([P, SHORT], F32, "short0")[:], 0, rounded0)
-        gather_and_round(0, tile([P, LONG], F32, "long0")[:], SHORT, rounded0)
+        q_woven = tile([P, Q * PACK], BF16, "q_woven")
+        nc.scalar.copy(q_woven[:].rearrange("p (q j) -> p q j", j=PACK), q_raw[:].rearrange("p j q -> p q j"))
+        rounded0 = place(pair_shape, BF16, "rounded0", IDENTITY + 1, 6)
+        gather_and_round(0, first_tenant(I, "whole0", SHORT1_ROUNDED), 0, rounded0)
         bank0 = turn(rounded0, "v0_bank", "bank_b")
-        rounded1 = tile(pair_shape, BF16, "rounded1")
-        gather_and_round(1, first_tenant(SHORT, "short1", SHORT1_ROUNDED), LONG, rounded1)
-        gather_and_round(1, tile([P, LONG], F32, "long1")[:], 0, rounded1)
-        woven01 = place(woven_shape, BF16, "woven01", SHORT1_ROUNDED, 2)
+        rounded1 = place(pair_shape, BF16, "rounded1", SHORT1_ROUNDED, 4)
+        gather_and_round(1, tile([P, I], F32, "whole1")[:], 0, rounded1)
+        woven01 = tile(woven_shape, BF16, "woven01")
         weave_values(woven01, 0, bank0)
         weave_values(woven01, 1, turn(rounded1, "v1_bank", "bank_c"))
 
-        picked_bytes = place([P, I], U8, "picked_bytes", SHORT1_ROUNDED)
-        nc.vector.tensor_copy(picked_bytes[:], key_bytes[:].indirect(key_list[:]))
-        picked_words = place([P, I], U32, "picked_words", BOOK0_TURNED)
+        q_codes, q_scales = quantise_stationary(q_woven, "q", place([P, Q], U32, "q_codes", SHORT1_ROUNDED, 2))
+        picked_words = place([P, I], U32, "picked_words", SHORT1_ROUNDED)
         nc.vector.tensor_copy(picked_words[:], key_words[:].bitcast(U32).indirect(key_list[:]))
-        q_woven = place([P, Q * PACK], BF16, "q_woven", BOOK0_TURNED, 2)
-        nc.scalar.copy(q_woven[:].rearrange("p (q j) -> p q j", j=PACK), q_raw[:].rearrange("p j q -> p q j"))
-        q_codes, q_scales = quantise_stationary(q_woven, "q")
-        scores = ps.tile([P, I], F32, name="scores")
+        scores = ps.tile([P, I], F32, name="scores", tag="bank_e")
         nc.tensor.matmul_mx(
             out=scores[:],
             lhsT=q_codes[:].bitcast(FP8X4),
             lhsT_scale=q_scales[:],
             rhs=picked_words[:].bitcast(FP8X4),
-            rhs_scale=picked_bytes[:],
+            rhs_scale=key_scales[:],
             start=True,
             stop=True,
         )
-        size_bank = spread(size_col, "size_bank", "bank_c")
+        size_bank = spread(size_col, "size_bank", "bank_f")
 
         rounded2 = tile(pair_shape, BF16, "rounded2")
         gather_and_round(2, first_tenant(SHORT, "short2", SHORT2_ROUNDED), 0, rounded2)
         gather_and_round(2, tile([P, LONG], F32, "long2")[:], SHORT, rounded2)
-        bank2 = turn(rounded2, "v2_bank", "bank_b")
 
         neg_max = place([P, 1], F32, "neg_max", SHORT2_ROUNDED, 4)
         nc.vector.tensor_reduce(neg_max[:], scores[:], AXIS.X, ALU.max, negate=True)
@@ -178,6 +172,7 @@ def tile_attend_pqvalues_kernel(tc, query, keys_words, keys_scales, vbook, size,
         scores_by_pair = scores[:].rearrange("q (n u s) -> q u n s", u=PAIRS, s=PAIR)
         nc.scalar.activation(probs[:], scores_by_pair, ACT.Exp, bias=neg_max[:], accum_out=row_sum[:])
 
+        bank2 = turn(rounded2, "v2_bank", "bank_e")
         rounded3 = place(pair_shape, BF16, "rounded3", SHORT2_ROUNDED, 4)
         for kib, (first, count) in enumerate(((0, I - 2 * SHORT), (I - 2 * SHORT, SHORT), (LONG, SHORT))):
             piece = place([P, count], F32, "piece3_%d" % kib, SHORT2_ROUNDED, kib)
@@ -210,7 +205,7 @@ def tile_attend_pqvalues_kernel(tc, query, keys_words, keys_scales, vbook, size,
             w_woven[:].bitcast(F32).rearrange("n (q u) -> n q u", u=PAIRS), w_bank[:].rearrange("n u q -> n q u")
         )
         quantise_values(woven23, 2)
-        w_codes, w_scales = quantise_stationary(w_woven, "w")
+        w_codes, w_scales = quantise_stationary(w_woven, "w", tile([P, Q], U32, "w_codes"))
 
         for h in range(HALVES):
             sums = ps.tile([P, PACK, HALF_P], F32, name="sums%d" % h)

@@ -69,7 +69,7 @@ def tile_attend_pqvalues_kernel(tc, query, keys_words, keys_scales, vbook, size,
         nc.sync.dma_start(key_list[:], offs)
         load_book(tile([P, C], F32, "book0"))
         nc.sync.dma_start(code_lists[:], offs2)
-        nc.sync.dma_start(key_bytes[0:P:8, :].bitcast(I32), keys_scales[0].bitcast(I32))
+        nc.scalar.dma_start(key_bytes[0:P:8, :].bitcast(I32), keys_scales[0].bitcast(I32))
         load_book(place([P, C], F32, "book1", IDENTITY + 1))
         q_raw = place([P, PACK, Q], F32, "q_raw", IDENTITY + 1, 6)
         nc.sync.dma_start(q_raw[:], query.rearrange("(p j) q -> p j q", j=PACK))

@@ -70,11 +70,11 @@ def tile_attend_pqvalues_kernel(tc, query, keys_words, keys_scales, vbook, size,
         load_book(tile([P, C], F32, "book0"))
         nc.sync.dma_start(code_lists[:], offs2)
         nc.scalar.dma_start(key_bytes[0:P:8, :].bitcast(I32), keys_scales[0].bitcast(I32))
+        key_words = place([P, T], I32, "key_words", IDENTITY)
+        nc.sync.dma_start(key_words[:], keys_words[0].rearrange("p n t -> p (n t)").bitcast(I32))
         load_book(place([P, C], F32, "book1", IDENTITY + 1))
         q_raw = place([P, PACK, Q], F32, "q_raw", IDENTITY + 1, 6)
         nc.sync.dma_start(q_raw[:], query.rearrange("(p j) q -> p j q", j=PACK))
-        key_words = place([P, T], I32, "key_words", IDENTITY)
-        nc.sync.dma_start(key_words[:], keys_words[0].rearrange("p n t -> p (n t)").bitcast(I32))
         picked_bytes = place([P, I], U8, "picked_bytes", IDENTITY + 1, 4)
         nc.vector.tensor_copy(picked_bytes[:], key_bytes.indirect(key_list[:]))
 
@@ -88,15 +88,14 @@ def tile_attend_pqvalues_kernel(tc, query, keys_words, keys_scales, vbook, size,
         vsc_row = tile([P, I], F32, "vsc_row")
         nc.scalar.copy(vsc_row[:].rearrange("p (n t) -> p n t", t=PACK), vsc_bank[:].rearrange("p t n -> p n t"))
         key_scales = tile([P, I], U8, "key_scales")
-        nc.vector.memset(key_scales[:].bitcast(I32), 0)
-        for quad in range(P // QUADRANT):
+        nc.vector.tensor_copy(key_scales[:].bitcast(I32), picked_bytes[:].bitcast(I32))
+        for row in range(1, PACK):
             nc.sync.dma_start(
-                key_scales[QUADRANT * quad : QUADRANT * quad + PACK, :].bitcast(I32),
-                picked_bytes[QUADRANT * quad : QUADRANT * (quad + 1) : 8, :].bitcast(I32),
+                key_scales[row:P:QUADRANT, :].bitcast(I32), picked_bytes[8 * row : P : QUADRANT, :].bitcast(I32)
             )
+        load_book(place([P, C], F32, "book2", BYTES_PICKED, 1))
         size_col = place([P, PACK], F32, "size_col", BYTES_PICKED)
         nc.sync.dma_start(size_col[:], size.rearrange("o (p t) -> p (o t)", t=PACK))
-        load_book(place([P, C], F32, "book2", BYTES_PICKED, 1))
         load_book(place([P, C], F32, "book3", BYTES_PICKED, 5))
 
         def gather_and_round(j, prod, first, rounded):
@@ -135,20 +134,17 @@ def tile_attend_pqvalues_kernel(tc, query, keys_words, keys_scales, vbook, size,
         pair_shape = [P, PAIRS, P, PAIR]
         woven_shape = [P, HALVES, 2, HALF_P * PACK]
 
-        q_woven = tile([P, Q * PACK], BF16, "q_woven")
-        nc.scalar.copy(q_woven[:].rearrange("p (q j) -> p q j", j=PACK), q_raw[:].rearrange("p j q -> p q j"))
-        rounded0 = place(pair_shape, BF16, "rounded0", IDENTITY + 1, 6)
-        gather_and_round(0, first_tenant(I, "whole0", SHORT1_ROUNDED), 0, rounded0)
+        rounded0 = tile(pair_shape, BF16, "rounded0")
+        gather_and_round(0, first_tenant(SHORT, "short0", SHORT1_ROUNDED), 0, rounded0)
+        gather_and_round(0, tile([P, LONG], F32, "long0")[:], SHORT, rounded0)
         bank0 = turn(rounded0, "v0_bank", "bank_b")
-        rounded1 = place(pair_shape, BF16, "rounded1", SHORT1_ROUNDED, 4)
-        gather_and_round(1, tile([P, I], F32, "whole1")[:], 0, rounded1)
-        woven01 = tile(woven_shape, BF16, "woven01")
-        weave_values(woven01, 0, bank0)
-        weave_values(woven01, 1, turn(rounded1, "v1_bank", "bank_c"))
-
-        q_codes, q_scales = quantise_stationary(q_woven, "q", place([P, Q], U32, "q_codes", SHORT1_ROUNDED, 2))
         picked_words = place([P, I], U32, "picked_words", SHORT1_ROUNDED)
         nc.vector.tensor_copy(picked_words[:], key_words[:].bitcast(U32).indirect(key_list[:]))
+        q_woven = place([P, Q * PACK], BF16, "q_woven", SHORT1_ROUNDED, 3)
+        nc.scalar.copy(q_woven[:].rearrange("p (q j) -> p q j", j=PACK), q_raw[:].rearrange("p j q -> p q j"))
+        rounded1 = place(pair_shape, BF16, "rounded1", IDENTITY + 1, 6)
+        gather_and_round(1, place([P, I], F32, "whole1", SHORT1_ROUNDED, 4)[:], 0, rounded1)
+        q_codes, q_scales = quantise_stationary(q_woven, "q", place([P, Q], U32, "q_codes", SHORT1_ROUNDED, 2))
         scores = ps.tile([P, I], F32, name="scores", tag="bank_e")
         nc.tensor.matmul_mx(
             out=scores[:],
@@ -162,7 +158,10 @@ def tile_attend_pqvalues_kernel(tc, query, keys_words, keys_scales, vbook, size,
         size_bank = spread(size_col, "size_bank", "bank_f")
 
         rounded2 = tile(pair_shape, BF16, "rounded2")
-        gather_and_round(2, first_tenant(SHORT, "short2", SHORT2_ROUNDED), 0, rounded2)
+        gather_and_round(2, place([P, 9 * KIB // 4], F32, "short2", IDENTITY + 1, 7)[:, 0:SHORT], 0, rounded2)
+        woven01 = place(woven_shape, BF16, "woven01", SHORT2_ROUNDED, 6)
+        weave_values(woven01, 0, bank0)
+        weave_values(woven01, 1, turn(rounded1, "v1_bank", "bank_b"))
         gather_and_round(2, tile([P, LONG], F32, "long2")[:], SHORT, rounded2)
 
         neg_max = place([P, 1], F32, "neg_max", SHORT2_ROUNDED, 4)

@@ -28,7 +28,7 @@ SHORT = 128
 LONG = I - SHORT
 KIB = 1024
 STRETCH = 8 * KIB
-IDENTITY, SHORT2_ROUNDED, SHORT1_ROUNDED, BOOK0_TURNED, BYTES_PICKED = 0, 2, 3, 4, 5
+IDENTITY, SHORT2_ROUNDED, SCORED, SHORT1_ROUNDED, LONG0_ROUNDED, BYTES_PICKED = 0, 2, 3, 4, 5, 6
 
 
 def tile_attend_pqvalues_kernel(tc, query, keys_words, keys_scales, vbook, size, vsc, offs, offs2, out):
@@ -42,7 +42,7 @@ def tile_attend_pqvalues_kernel(tc, query, keys_words, keys_scales, vbook, size,
             return sb.tile(shape, dtype, name=name, tag=tag or name, align_bytes=64)
 
         def place(shape, dtype, name, stretch, kib=0):
-            return placed.tile(shape, dtype, name=name, offset=stretch * STRETCH + kib * KIB, align_bytes=64)
+            return placed.tile(shape, dtype, name=name, offset=stretch * STRETCH + int(kib * KIB), align_bytes=64)
 
         def first_tenant(columns, name, stretch, stretches=1):
             return place([P, stretches * STRETCH // 4], F32, name, stretch)[:, 0:columns]
@@ -87,16 +87,7 @@ def tile_attend_pqvalues_kernel(tc, query, keys_words, keys_scales, vbook, size,
         vsc_bank = spread(vsc_col, "vsc_bank", "bank_a")
         vsc_row = tile([P, I], F32, "vsc_row")
         nc.scalar.copy(vsc_row[:].rearrange("p (n t) -> p n t", t=PACK), vsc_bank[:].rearrange("p t n -> p n t"))
-        key_scales = tile([P, I], U8, "key_scales")
-        nc.vector.tensor_copy(key_scales[:].bitcast(I32), picked_bytes[:].bitcast(I32))
-        for row in range(1, PACK):
-            nc.sync.dma_start(
-                key_scales[row:P:QUADRANT, :].bitcast(I32), picked_bytes[8 * row : P : QUADRANT, :].bitcast(I32)
-            )
-        load_book(place([P, C], F32, "book2", BYTES_PICKED, 1))
-        size_col = place([P, PACK], F32, "size_col", BYTES_PICKED)
-        nc.sync.dma_start(size_col[:], size.rearrange("o (p t) -> p (o t)", t=PACK))
-        load_book(place([P, C], F32, "book3", BYTES_PICKED, 5))
+        load_book(place([P, C], F32, "book2", BYTES_PICKED))
 
         def gather_and_round(j, prod, first, rounded):
             count = prod.shape[1]
@@ -112,17 +103,18 @@ def tile_attend_pqvalues_kernel(tc, query, keys_words, keys_scales, vbook, size,
                 nc.tensor.transpose(bank[:, u, :], words, ident[:])
             return bank
 
-        def weave_values(woven, j, bank):
+        def weave_values(woven, place_in_tile, bank):
             nc.scalar.copy(
-                woven[:, :, j % 2, :].bitcast(F32).rearrange("n h (r u) -> n h r u", u=PAIRS),
+                woven[:, :, place_in_tile, :].bitcast(F32).rearrange("n h (r u) -> n h r u", u=PAIRS),
                 bank[:].rearrange("n u (h r) -> n h r u", h=HALVES),
             )
 
         def quantise_values(woven, first):
+            books_here = slice(first, first + woven.shape[2])
             for h in range(HALVES):
                 nc.vector.quantize_mx(
-                    out=v_codes[:, h, first : first + 2, :].rearrange("n j r -> n (j r)").bitcast(FP8X4),
-                    scales=v_scales[:, h, first : first + 2, :].rearrange("n j r -> n (j r)"),
+                    out=v_codes[:, h, books_here, :].rearrange("n j r -> n (j r)").bitcast(FP8X4),
+                    scales=v_scales[:, h, books_here, :].rearrange("n j r -> n (j r)"),
                     in_=woven[:, h, :, :].rearrange("n j r -> n (j r)"),
                 )
 
@@ -132,14 +124,22 @@ def tile_attend_pqvalues_kernel(tc, query, keys_words, keys_scales, vbook, size,
             return codes, scales
 
         pair_shape = [P, PAIRS, P, PAIR]
-        woven_shape = [P, HALVES, 2, HALF_P * PACK]
 
         rounded0 = tile(pair_shape, BF16, "rounded0")
-        gather_and_round(0, first_tenant(SHORT, "short0", SHORT1_ROUNDED), 0, rounded0)
-        gather_and_round(0, tile([P, LONG], F32, "long0")[:], SHORT, rounded0)
+        gather_and_round(0, first_tenant(SHORT, "short0", SCORED, 2), 0, rounded0)
+        gather_and_round(0, first_tenant(LONG, "long0", LONG0_ROUNDED), SHORT, rounded0)
+        key_scales = place([P, I], U8, "key_scales", SHORT1_ROUNDED, 7)
+        nc.vector.tensor_copy(key_scales[:].bitcast(I32), picked_bytes[:].bitcast(I32))
+        for row in range(1, PACK):
+            nc.sync.dma_start(
+                key_scales[row:P:QUADRANT, :].bitcast(I32), picked_bytes[8 * row : P : QUADRANT, :].bitcast(I32)
+            )
+        size_col = place([P, PACK], F32, "size_col", LONG0_ROUNDED)
+        nc.sync.dma_start(size_col[:], size.rearrange("o (p t) -> p (o t)", t=PACK))
+        load_book(place([P, C], F32, "book3", LONG0_ROUNDED, 4))
         bank0 = turn(rounded0, "v0_bank", "bank_b")
-        picked_words = place([P, I], U32, "picked_words", SHORT1_ROUNDED)
-        nc.vector.tensor_copy(picked_words[:], key_words[:].bitcast(U32).indirect(key_list[:]))
+        picked_words = place([P, STRETCH // 4], U32, "picked_words", SCORED)[:, 0:I]
+        nc.vector.tensor_copy(picked_words, key_words[:].bitcast(U32).indirect(key_list[:]))
         q_woven = place([P, Q * PACK], BF16, "q_woven", SHORT1_ROUNDED, 3)
         nc.scalar.copy(q_woven[:].rearrange("p (q j) -> p q j", j=PACK), q_raw[:].rearrange("p j q -> p q j"))
         rounded1 = place(pair_shape, BF16, "rounded1", IDENTITY + 1, 6)
@@ -150,7 +150,7 @@ def tile_attend_pqvalues_kernel(tc, query, keys_words, keys_scales, vbook, size,
             out=scores[:],
             lhsT=q_codes[:].bitcast(FP8X4),
             lhsT_scale=q_scales[:],
-            rhs=picked_words[:].bitcast(FP8X4),
+            rhs=picked_words.bitcast(FP8X4),
             rhs_scale=key_scales[:],
             start=True,
             stop=True,
@@ -159,12 +159,12 @@ def tile_attend_pqvalues_kernel(tc, query, keys_words, keys_scales, vbook, size,
 
         rounded2 = tile(pair_shape, BF16, "rounded2")
         gather_and_round(2, place([P, 9 * KIB // 4], F32, "short2", IDENTITY + 1, 7)[:, 0:SHORT], 0, rounded2)
-        woven01 = place(woven_shape, BF16, "woven01", SHORT2_ROUNDED, 6)
-        weave_values(woven01, 0, bank0)
-        weave_values(woven01, 1, turn(rounded1, "v1_bank", "bank_b"))
+        woven0 = place([P, HALVES, 1, HALF_P * PACK], BF16, "woven0", SHORT2_ROUNDED, 7.5)
+        weave_values(woven0, 0, bank0)
+        bank1 = turn(rounded1, "v1_bank", "bank_b")
         gather_and_round(2, tile([P, LONG], F32, "long2")[:], SHORT, rounded2)
 
-        neg_max = place([P, 1], F32, "neg_max", SHORT2_ROUNDED, 4)
+        neg_max = place([P, 1], F32, "neg_max", SCORED, 7)
         nc.vector.tensor_reduce(neg_max[:], scores[:], AXIS.X, ALU.max, negate=True)
         probs = tile(pair_shape, F32, "probs")
         row_sum = tile([P, 1], F32, "row_sum")
@@ -172,13 +172,14 @@ def tile_attend_pqvalues_kernel(tc, query, keys_words, keys_scales, vbook, size,
         nc.scalar.activation(probs[:], scores_by_pair, ACT.Exp, bias=neg_max[:], accum_out=row_sum[:])
 
         bank2 = turn(rounded2, "v2_bank", "bank_e")
-        rounded3 = place(pair_shape, BF16, "rounded3", SHORT2_ROUNDED, 4)
+        rounded3 = place(pair_shape, BF16, "rounded3", SCORED, 7)
         for kib, (first, count) in enumerate(((0, I - 2 * SHORT), (I - 2 * SHORT, SHORT), (LONG, SHORT))):
-            piece = place([P, count], F32, "piece3_%d" % kib, SHORT2_ROUNDED, kib)
+            piece = place([P, count], F32, "piece3_%d" % kib, SCORED, 2 + kib)
             gather_and_round(3, piece[:], first, rounded3)
         bank3 = turn(rounded3, "v3_bank", "bank_d")
-        woven23 = place(woven_shape, BF16, "woven23", SHORT2_ROUNDED, 2)
-        weave_values(woven23, 2, bank2)
+        woven12 = place([P, HALVES, 2, HALF_P * PACK], BF16, "woven12", SCORED, 4)
+        weave_values(woven12, 0, bank1)
+        weave_values(woven12, 1, bank2)
 
         inv_sum = tile([P, 1], F32, "inv_sum")
         nc.vector.reciprocal(inv_sum[:], row_sum[:])
@@ -194,16 +195,18 @@ def tile_attend_pqvalues_kernel(tc, query, keys_words, keys_scales, vbook, size,
                 ALU.mult,
             )
             nc.tensor.transpose(w_bank[:, u, :], weights[:].rearrange("q n s -> q (n s)").bitcast(F32), ident[:])
-        weave_values(woven23, 3, bank3)
+        woven3 = tile([P, HALVES, 1, HALF_P * PACK], BF16, "woven3")
+        weave_values(woven3, 0, bank3)
 
         v_codes = tile([P, HALVES, PACK, HALF_P], U32, "v_codes", "probs")
         v_scales = tile([P, HALVES, PACK, HALF_P], U8, "v_scales")
-        quantise_values(woven01, 0)
+        quantise_values(woven0, 0)
+        quantise_values(woven12, 1)
         w_woven = tile([P, Q * PACK], BF16, "w_woven")
         nc.scalar.copy(
             w_woven[:].bitcast(F32).rearrange("n (q u) -> n q u", u=PAIRS), w_bank[:].rearrange("n u q -> n q u")
         )
-        quantise_values(woven23, 2)
+        quantise_values(woven3, 3)
         w_codes, w_scales = quantise_stationary(w_woven, "w", tile([P, Q], U32, "w_codes"))
 
         for h in range(HALVES):

@@ -61,15 +61,15 @@ def tile_attend_pqvalues_kernel(tc, query, keys_words, keys_scales, vbook, size,
         book_rows = vbook.rearrange("(p j) c -> j p c", j=PACK)
         books = []
 
-        def load_book(book):
-            nc.sync.dma_start(book[:], book_rows[len(books)])
+        def load_book(book, queue=nc.sync):
+            queue.dma_start(book[:], book_rows[len(books)])
             books.append(book)
 
-        nc.scalar.dma_start(vsc_col, vsc.rearrange("(p t) o -> p (t o)", t=PACK))
+        load_book(tile([P, C], F32, "book0"), nc.scalar)
+        nc.sync.dma_start(vsc_col, vsc.rearrange("(p t) o -> p (t o)", t=PACK))
         nc.sync.dma_start(key_list[:], offs)
-        load_book(tile([P, C], F32, "book0"))
         nc.sync.dma_start(code_lists[:], offs2)
-        nc.scalar.dma_start(key_bytes[0:P:8, :].bitcast(I32), keys_scales[0].bitcast(I32))
+        nc.sync.dma_start(key_bytes[0:P:8, :].bitcast(I32), keys_scales[0].bitcast(I32))
         key_words = place([P, T], I32, "key_words", IDENTITY)
         nc.sync.dma_start(key_words[:], keys_words[0].rearrange("p n t -> p (n t)").bitcast(I32))
         load_book(place([P, C], F32, "book1", IDENTITY + 1))

@@ -21,6 +21,7 @@ PACK = 4
 PAIR = 2
 PAIRS = PACK // PAIR
 GROUP = 16
+BLOCK = 8
 QUADRANT = 32
 HALVES = 2
 HALF_P = P // HALVES
@@ -28,7 +29,8 @@ SHORT = 128
 LONG = I - SHORT
 KIB = 1024
 STRETCH = 8 * KIB
-IDENTITY, SHORT2_ROUNDED, SCORED, SHORT1_ROUNDED, LONG0_ROUNDED, BYTES_PICKED = 0, 2, 3, 4, 5, 6
+IDENTITY, SCORED, SHORT0_ROUNDED, LONG0_ROUNDED, BYTES_PICKED = 0, 3, 4, 5, 6
+QUERIES_KIB = 14
 
 
 def tile_attend_pqvalues_kernel(tc, query, keys_words, keys_scales, vbook, size, vsc, offs, offs2, out):
@@ -42,14 +44,14 @@ def tile_attend_pqvalues_kernel(tc, query, keys_words, keys_scales, vbook, size,
             return sb.tile(shape, dtype, name=name, tag=tag or name, align_bytes=64)
 
         def place(shape, dtype, name, stretch, kib=0):
-            return placed.tile(shape, dtype, name=name, offset=stretch * STRETCH + int(kib * KIB), align_bytes=64)
+            return placed.tile(shape, dtype, name=name, offset=stretch * STRETCH + kib * KIB, align_bytes=64)
 
         def first_tenant(columns, name, stretch, stretches=1):
             return place([P, stretches * STRETCH // 4], F32, name, stretch)[:, 0:columns]
 
         key_list = sb.tile([P, I // GROUP], U16, name="key_list")
         code_lists = sb.tile([P, I // GROUP], U16, name="code_lists")
-        vsc_col = tile([P, PACK], F32, "vsc_col")[:]
+        vsc_col = tile([P, PACK], F32, "vsc_col")
         key_bytes = place([P, 2 * STRETCH], U8, "key_bytes", BYTES_PICKED)[:, 0:T]
         ident = tile([P, P], F32, "ident")
 
@@ -66,16 +68,16 @@ def tile_attend_pqvalues_kernel(tc, query, keys_words, keys_scales, vbook, size,
             books.append(book)
 
         load_book(tile([P, C], F32, "book0"), nc.scalar)
-        nc.sync.dma_start(vsc_col, vsc.rearrange("(p t) o -> p (t o)", t=PACK))
+        nc.sync.dma_start(vsc_col[:], vsc.rearrange("(p t) o -> p (t o)", t=PACK))
         nc.sync.dma_start(key_list[:], offs)
         nc.sync.dma_start(code_lists[:], offs2)
-        nc.sync.dma_start(key_bytes[0:P:8, :].bitcast(I32), keys_scales[0].bitcast(I32))
+        nc.sync.dma_start(key_bytes[0:P:BLOCK, :].bitcast(I32), keys_scales[0].bitcast(I32))
         key_words = place([P, T], I32, "key_words", IDENTITY)
         nc.sync.dma_start(key_words[:], keys_words[0].rearrange("p n t -> p (n t)").bitcast(I32))
-        load_book(place([P, C], F32, "book1", IDENTITY + 1))
-        q_raw = place([P, PACK, Q], F32, "q_raw", IDENTITY + 1, 6)
+        load_book(place([P, C], F32, "book1", IDENTITY, 8))
+        q_raw = place([P, PACK, Q], F32, "q_raw", IDENTITY, QUERIES_KIB)
         nc.sync.dma_start(q_raw[:], query.rearrange("(p j) q -> p j q", j=PACK))
-        picked_bytes = place([P, I], U8, "picked_bytes", IDENTITY + 1, 4)
+        picked_bytes = place([P, I], U8, "picked_bytes", IDENTITY, 12)
         nc.vector.tensor_copy(picked_bytes[:], key_bytes.indirect(key_list[:]))
 
         def spread(col, name, tag):
@@ -103,18 +105,21 @@ def tile_attend_pqvalues_kernel(tc, query, keys_words, keys_scales, vbook, size,
                 nc.tensor.transpose(bank[:, u, :], words, ident[:])
             return bank
 
-        def weave_values(woven, place_in_tile, bank):
+        def woven_shape(count):
+            return [P, HALVES, count, HALF_P * PACK]
+
+        def weave_values(woven, which, bank):
             nc.scalar.copy(
-                woven[:, :, place_in_tile, :].bitcast(F32).rearrange("n h (r u) -> n h r u", u=PAIRS),
+                woven[:, :, which, :].bitcast(F32).rearrange("n h (r u) -> n h r u", u=PAIRS),
                 bank[:].rearrange("n u (h r) -> n h r u", h=HALVES),
             )
 
         def quantise_values(woven, first):
-            books_here = slice(first, first + woven.shape[2])
+            these = slice(first, first + woven.shape[2])
             for h in range(HALVES):
                 nc.vector.quantize_mx(
-                    out=v_codes[:, h, books_here, :].rearrange("n j r -> n (j r)").bitcast(FP8X4),
-                    scales=v_scales[:, h, books_here, :].rearrange("n j r -> n (j r)"),
+                    out=v_codes[:, h, these, :].rearrange("n j r -> n (j r)").bitcast(FP8X4),
+                    scales=v_scales[:, h, these, :].rearrange("n j r -> n (j r)"),
                     in_=woven[:, h, :, :].rearrange("n j r -> n (j r)"),
                 )
 
@@ -128,23 +133,25 @@ def tile_attend_pqvalues_kernel(tc, query, keys_words, keys_scales, vbook, size,
         rounded0 = tile(pair_shape, BF16, "rounded0")
         gather_and_round(0, first_tenant(SHORT, "short0", SCORED, 2), 0, rounded0)
         gather_and_round(0, first_tenant(LONG, "long0", LONG0_ROUNDED), SHORT, rounded0)
-        key_scales = place([P, I], U8, "key_scales", SHORT1_ROUNDED, 7)
+
+        key_scales = place([P, I], U8, "key_scales", SHORT0_ROUNDED, 7)
         nc.vector.tensor_copy(key_scales[:].bitcast(I32), picked_bytes[:].bitcast(I32))
-        for row in range(1, PACK):
+        for r in range(1, PACK):
             nc.sync.dma_start(
-                key_scales[row:P:QUADRANT, :].bitcast(I32), picked_bytes[8 * row : P : QUADRANT, :].bitcast(I32)
+                key_scales[r:P:QUADRANT, :].bitcast(I32), picked_bytes[BLOCK * r : P : QUADRANT, :].bitcast(I32)
             )
         size_col = place([P, PACK], F32, "size_col", LONG0_ROUNDED)
         nc.sync.dma_start(size_col[:], size.rearrange("o (p t) -> p (o t)", t=PACK))
         load_book(place([P, C], F32, "book3", LONG0_ROUNDED, 4))
         bank0 = turn(rounded0, "v0_bank", "bank_b")
+
         picked_words = place([P, STRETCH // 4], U32, "picked_words", SCORED)[:, 0:I]
         nc.vector.tensor_copy(picked_words, key_words[:].bitcast(U32).indirect(key_list[:]))
-        q_woven = place([P, Q * PACK], BF16, "q_woven", SHORT1_ROUNDED, 3)
+        q_woven = place([P, Q * PACK], BF16, "q_woven", SHORT0_ROUNDED, 3)
         nc.scalar.copy(q_woven[:].rearrange("p (q j) -> p q j", j=PACK), q_raw[:].rearrange("p j q -> p q j"))
-        rounded1 = place(pair_shape, BF16, "rounded1", IDENTITY + 1, 6)
-        gather_and_round(1, place([P, I], F32, "whole1", SHORT1_ROUNDED, 4)[:], 0, rounded1)
-        q_codes, q_scales = quantise_stationary(q_woven, "q", place([P, Q], U32, "q_codes", SHORT1_ROUNDED, 2))
+        rounded1 = place(pair_shape, BF16, "rounded1", IDENTITY, QUERIES_KIB)
+        gather_and_round(1, place([P, I], F32, "whole1", SHORT0_ROUNDED, 4)[:], 0, rounded1)
+        q_codes, q_scales = quantise_stationary(q_woven, "q", place([P, Q], U32, "q_codes", SHORT0_ROUNDED, 2))
         scores = ps.tile([P, I], F32, name="scores", tag="bank_e")
         nc.tensor.matmul_mx(
             out=scores[:],
@@ -158,11 +165,10 @@ def tile_attend_pqvalues_kernel(tc, query, keys_words, keys_scales, vbook, size,
         size_bank = spread(size_col, "size_bank", "bank_f")
 
         rounded2 = tile(pair_shape, BF16, "rounded2")
-        gather_and_round(2, place([P, 9 * KIB // 4], F32, "short2", IDENTITY + 1, 7)[:, 0:SHORT], 0, rounded2)
-        woven0 = place([P, HALVES, 1, HALF_P * PACK], BF16, "woven0", SHORT2_ROUNDED, 7.5)
+        gather_and_round(2, place([P, I], F32, "whole2", IDENTITY, QUERIES_KIB + 1)[:], 0, rounded2)
+        woven0 = place(woven_shape(1), BF16, "woven0", SCORED)
         weave_values(woven0, 0, bank0)
         bank1 = turn(rounded1, "v1_bank", "bank_b")
-        gather_and_round(2, tile([P, LONG], F32, "long2")[:], SHORT, rounded2)
 
         neg_max = place([P, 1], F32, "neg_max", SCORED, 7)
         nc.vector.tensor_reduce(neg_max[:], scores[:], AXIS.X, ALU.max, negate=True)
@@ -170,14 +176,15 @@ def tile_attend_pqvalues_kernel(tc, query, keys_words, keys_scales, vbook, size,
         row_sum = tile([P, 1], F32, "row_sum")
         scores_by_pair = scores[:].rearrange("q (n u s) -> q u n s", u=PAIRS, s=PAIR)
         nc.scalar.activation(probs[:], scores_by_pair, ACT.Exp, bias=neg_max[:], accum_out=row_sum[:])
-
         bank2 = turn(rounded2, "v2_bank", "bank_e")
-        rounded3 = place(pair_shape, BF16, "rounded3", SCORED, 7)
-        for kib, (first, count) in enumerate(((0, I - 2 * SHORT), (I - 2 * SHORT, SHORT), (LONG, SHORT))):
-            piece = place([P, count], F32, "piece3_%d" % kib, SCORED, 2 + kib)
+
+        rounded3 = tile(pair_shape, BF16, "rounded3")
+        pieces = ((0, I - 2 * SHORT), (I - 2 * SHORT, SHORT), (LONG, SHORT))
+        for number, (first, count) in enumerate(pieces):
+            piece = place([P, count], F32, "piece3_%d" % number, SCORED, 2 + number)
             gather_and_round(3, piece[:], first, rounded3)
         bank3 = turn(rounded3, "v3_bank", "bank_d")
-        woven12 = place([P, HALVES, 2, HALF_P * PACK], BF16, "woven12", SCORED, 4)
+        woven12 = place(woven_shape(2), BF16, "woven12", SCORED, 1 + len(pieces))
         weave_values(woven12, 0, bank1)
         weave_values(woven12, 1, bank2)
 
@@ -195,7 +202,7 @@ def tile_attend_pqvalues_kernel(tc, query, keys_words, keys_scales, vbook, size,
                 ALU.mult,
             )
             nc.tensor.transpose(w_bank[:, u, :], weights[:].rearrange("q n s -> q (n s)").bitcast(F32), ident[:])
-        woven3 = tile([P, HALVES, 1, HALF_P * PACK], BF16, "woven3")
+        woven3 = tile(woven_shape(1), BF16, "woven3")
         weave_values(woven3, 0, bank3)
 
         v_codes = tile([P, HALVES, PACK, HALF_P], U32, "v_codes", "probs")

@@ -25,12 +25,9 @@ BLOCK = 8
 QUADRANT = 32
 HALVES = 2
 HALF_P = P // HALVES
+HALF_I = I // 2
 SHORT = 128
-LONG = I - SHORT
 KIB = 1024
-STRETCH = 8 * KIB
-IDENTITY, SCORED, SHORT0_ROUNDED, LONG0_ROUNDED, BYTES_PICKED = 0, 3, 4, 5, 6
-QUERIES_KIB = 14
 
 
 def tile_attend_pqvalues_kernel(tc, query, keys_words, keys_scales, vbook, size, vsc, offs, offs2, out):
@@ -39,80 +36,128 @@ def tile_attend_pqvalues_kernel(tc, query, keys_words, keys_scales, vbook, size,
         sb = ctx.enter_context(tc.tile_pool(name="sb", bufs=1))
         placed = ctx.enter_context(tc.tile_pool(name="placed", bufs=1))
         ps = ctx.enter_context(tc.psum_pool(name="ps", bufs=1))
+        free = {"": (0, 200 * KIB)}
 
-        def tile(shape, dtype, name, tag=None):
-            return sb.tile(shape, dtype, name=name, tag=tag or name, align_bytes=64)
-
-        def place(shape, dtype, name, stretch, kib=0):
-            return placed.tile(shape, dtype, name=name, offset=stretch * STRETCH + kib * KIB, align_bytes=64)
-
-        def first_tenant(columns, name, stretch, stretches=1):
-            return place([P, stretches * STRETCH // 4], F32, name, stretch)[:, 0:columns]
+        def tile(shape, dtype, name, behind="", room_kib=0):
+            width = 4 if dtype in (F32, I32, U32) else 2 if dtype == BF16 else 1
+            columns = 1
+            for extent in shape[1:]:
+                columns = columns * extent
+            span = max(room_kib * KIB, -(-columns * width // 64) * 64)
+            start, end = free[behind]
+            assert start + span <= end
+            free[behind] = (start + span, end)
+            free[name] = (start, start + span)
+            if room_kib == 0:
+                return placed.tile(shape, dtype, name=name, offset=start, align_bytes=64)[:]
+            assert len(shape) == 2
+            return placed.tile([P, span // width], dtype, name=name, offset=start, align_bytes=64)[:, 0:columns]
 
         key_list = sb.tile([P, I // GROUP], U16, name="key_list")
         code_lists = sb.tile([P, I // GROUP], U16, name="code_lists")
-        vsc_col = tile([P, PACK], F32, "vsc_col")
-        key_bytes = place([P, 2 * STRETCH], U8, "key_bytes", BYTES_PICKED)[:, 0:T]
+        key_bytes = tile([P, T], U8, "key_bytes", room_kib=10)
         ident = tile([P, P], F32, "ident")
 
         nc.vector.memset(key_bytes.bitcast(I32), 0)
-        distance = first_tenant(P, "distance", IDENTITY, 2)
+        key_scales = tile([P, I], U8, "key_scales")
+        nc.vector.memset(key_scales.bitcast(I32), 0)
+        distance = tile([P, P], F32, "distance", room_kib=20)
         nc.gpsimd.iota(distance, [[1, P]], base=0, channel_multiplier=-1, allow_small_or_imprecise_dtypes=True)
-        nc.vector.tensor_scalar(ident[:], distance, 0.0, None, ALU.is_equal)
+        nc.vector.tensor_scalar(ident, distance, 0.0, None, ALU.is_equal)
 
         book_rows = vbook.rearrange("(p j) c -> j p c", j=PACK)
         books = []
 
-        def load_book(book, queue=nc.sync):
-            queue.dma_start(book[:], book_rows[len(books)])
+        def load_book(behind, queue=nc.sync):
+            book = tile([P, C], F32, "book%d" % len(books), behind)
+            queue.dma_start(book, book_rows[len(books)])
             books.append(book)
 
-        load_book(tile([P, C], F32, "book0"), nc.scalar)
-        nc.sync.dma_start(vsc_col[:], vsc.rearrange("(p t) o -> p (t o)", t=PACK))
+        load_book("", nc.scalar)
+        vsc_col = tile([P, PACK], F32, "vsc_col", room_kib=2)
+        nc.sync.dma_start(vsc_col, vsc.rearrange("(p t) o -> p (t o)", t=PACK))
         nc.sync.dma_start(key_list[:], offs)
         nc.sync.dma_start(code_lists[:], offs2)
         nc.sync.dma_start(key_bytes[0:P:BLOCK, :].bitcast(I32), keys_scales[0].bitcast(I32))
-        key_words = place([P, T], I32, "key_words", IDENTITY)
-        nc.sync.dma_start(key_words[:], keys_words[0].rearrange("p n t -> p (n t)").bitcast(I32))
-        load_book(place([P, C], F32, "book1", IDENTITY, 8))
-        q_raw = place([P, PACK, Q], F32, "q_raw", IDENTITY, QUERIES_KIB)
-        nc.sync.dma_start(q_raw[:], query.rearrange("(p j) q -> p j q", j=PACK))
-        picked_bytes = place([P, I], U8, "picked_bytes", IDENTITY, 12)
-        nc.vector.tensor_copy(picked_bytes[:], key_bytes.indirect(key_list[:]))
+        key_words = tile([P, T], I32, "key_words", "distance")
+        nc.sync.dma_start(key_words, keys_words[0].rearrange("p n t -> p (n t)").bitcast(I32))
+        q_raw = tile([P, PACK * Q], F32, "q_raw", "distance")
+        nc.sync.dma_start(q_raw.rearrange("p (j q) -> p j q", j=PACK), query.rearrange("(p j) q -> p j q", j=PACK))
+        load_book("distance")
+
+        picked_bytes = tile([P, I], U8, "picked_bytes", "distance")
+        nc.vector.tensor_copy(picked_bytes, key_bytes.indirect(key_list[:]))
+        for r in range(PACK):
+            nc.sync.dma_start(
+                key_scales[r:P:QUADRANT, :].bitcast(I32), picked_bytes[BLOCK * r : P : QUADRANT, :].bitcast(I32)
+            )
+        size_col = tile([P, PACK], F32, "size_col", "key_bytes")
+        nc.sync.dma_start(size_col, size.rearrange("o (p t) -> p (o t)", t=PACK))
+        load_book("key_bytes")
+        load_book("key_bytes")
 
         def spread(col, name, tag):
             bank = ps.tile([P, PACK, P], F32, name=name, tag=tag)
             for t in range(PACK):
-                nc.tensor.transpose(bank[:, t, :], col[:, t : t + 1].to_broadcast([P, P]), ident[:])
+                nc.tensor.transpose(bank[:, t, :], col[:, t : t + 1].to_broadcast([P, P]), ident)
             return bank
 
+        vsc_kept = tile([P, PACK], F32, "vsc_kept")
+        nc.gpsimd.tensor_copy(vsc_kept, vsc_col)
         vsc_bank = spread(vsc_col, "vsc_bank", "bank_a")
-        vsc_row = tile([P, I], F32, "vsc_row")
-        nc.scalar.copy(vsc_row[:].rearrange("p (n t) -> p n t", t=PACK), vsc_bank[:].rearrange("p t n -> p n t"))
-        load_book(place([P, C], F32, "book2", BYTES_PICKED))
 
-        def gather_and_round(j, prod, first, rounded):
-            count = prod.shape[1]
-            lists = code_lists[:, first // GROUP : (first + count) // GROUP]
-            nc.vector.tensor_tensor(prod, books[j][:].indirect(lists), vsc_row[:, first : first + count], ALU.mult)
-            rows = slice(first // PACK, (first + count) // PACK)
-            nc.scalar.copy(rounded[:, :, rows, :], prod.rearrange("p (n u s) -> p u n s", u=PAIRS, s=PAIR))
+
+        def vsc_half(first, name, room_kib=0):
+            row = tile([P, HALF_I], F32, name, "", room_kib)
+            rows = slice(first // PACK, (first + HALF_I) // PACK)
+            nc.scalar.copy(row.rearrange("p (n t) -> p n t", t=PACK), vsc_bank[:, :, rows].rearrange("p t n -> p n t"))
+            return row
+
+        vsc_low = vsc_half(0, "vsc_low", 4)
+
+        def by_pair(columns):
+            return columns.rearrange("p (n u s) -> p u n s", u=PAIRS, s=PAIR)
+
+        def listed(j, first, count):
+            return books[j].indirect(code_lists[:, first // GROUP : (first + count) // GROUP])
+
+        def slots(rounded, first, count):
+            return rounded[:, :, first // PACK : (first + count) // PACK, :]
+
+        def vector_gather(j, first, factors, name, behind="", room_kib=0):
+            count = factors.shape[1]
+            prod = tile([P, count], F32, name, behind, room_kib)
+            nc.vector.tensor_tensor(prod, listed(j, first, count), factors, ALU.mult)
+            return prod
+
+        def scalar_gather(j, first, count, name, behind="", room_kib=0):
+            raw = tile([P, count], F32, name, behind, room_kib)
+            nc.scalar.activation(raw, listed(j, first, count), ACT.Copy)
+            return raw
+
+        def scalar_round(rounded, prod, first):
+            nc.scalar.copy(slots(rounded, first, prod.shape[1]), by_pair(prod))
+
+        def vector_round(rounded, raw, first):
+            count = raw.shape[1]
+            factors = vsc_bank[:].rearrange("p (u s) n -> p u n s", s=PAIR)
+            nc.vector.tensor_tensor(slots(rounded, first, count), by_pair(raw), slots(factors, first, count), ALU.mult)
 
         def turn(rounded, name, tag):
             bank = ps.tile([P, PAIRS, P], F32, name=name, tag=tag)
             for u in range(PAIRS):
                 words = rounded[:, u].rearrange("p n s -> p (n s)").bitcast(F32)
-                nc.tensor.transpose(bank[:, u, :], words, ident[:])
+                nc.tensor.transpose(bank[:, u, :], words, ident)
             return bank
 
-        def woven_shape(count):
-            return [P, HALVES, count, HALF_P * PACK]
-
-        def weave_values(woven, which, bank):
-            nc.scalar.copy(
-                woven[:, :, which, :].bitcast(F32).rearrange("n h (r u) -> n h r u", u=PAIRS),
+        def weave(bank, woven, copy=nc.scalar.copy):
+            copy(
+                woven.bitcast(F32).rearrange("n h (r u) -> n h r u", u=PAIRS),
                 bank[:].rearrange("n u (h r) -> n h r u", h=HALVES),
             )
+
+        def woven_tile(count, name, behind=""):
+            return tile([P, HALVES, count, HALF_P * PACK], BF16, name, behind)
 
         def quantise_values(woven, first):
             these = slice(first, first + woven.shape[2])
@@ -123,105 +168,102 @@ def tile_attend_pqvalues_kernel(tc, query, keys_words, keys_scales, vbook, size,
                     in_=woven[:, h, :, :].rearrange("n j r -> n (j r)"),
                 )
 
-        def quantise_stationary(woven, name, codes):
+        def quantise_stationary(woven, name, behind=""):
+            codes = tile([P, Q], U32, name + "_codes", behind)
             scales = tile([P, Q], U8, name + "_scales")
-            nc.vector.quantize_mx(out=codes[:].bitcast(FP8X4), scales=scales[:], in_=woven[:])
+            nc.vector.quantize_mx(out=codes.bitcast(FP8X4), scales=scales, in_=woven)
             return codes, scales
 
         pair_shape = [P, PAIRS, P, PAIR]
 
-        rounded0 = tile(pair_shape, BF16, "rounded0")
-        gather_and_round(0, first_tenant(SHORT, "short0", SCORED, 2), 0, rounded0)
-        gather_and_round(0, first_tenant(LONG, "long0", LONG0_ROUNDED), SHORT, rounded0)
-
-        key_scales = place([P, I], U8, "key_scales", SHORT0_ROUNDED, 7)
-        nc.vector.tensor_copy(key_scales[:].bitcast(I32), picked_bytes[:].bitcast(I32))
-        for r in range(1, PACK):
-            nc.sync.dma_start(
-                key_scales[r:P:QUADRANT, :].bitcast(I32), picked_bytes[BLOCK * r : P : QUADRANT, :].bitcast(I32)
-            )
-        size_col = place([P, PACK], F32, "size_col", LONG0_ROUNDED)
-        nc.sync.dma_start(size_col[:], size.rearrange("o (p t) -> p (o t)", t=PACK))
-        load_book(place([P, C], F32, "book3", LONG0_ROUNDED, 4))
+        rounded0 = tile(pair_shape, BF16, "rounded0", "key_bytes")
+        raw0 = scalar_gather(0, 0, I, "raw0", "vsc_col")
+        vsc_high = vsc_half(HALF_I, "vsc_high")
+        vector_round(rounded0, raw0, 0)
         bank0 = turn(rounded0, "v0_bank", "bank_b")
 
-        picked_words = place([P, STRETCH // 4], U32, "picked_words", SCORED)[:, 0:I]
-        nc.vector.tensor_copy(picked_words, key_words[:].bitcast(U32).indirect(key_list[:]))
-        q_woven = place([P, Q * PACK], BF16, "q_woven", SHORT0_ROUNDED, 3)
-        nc.scalar.copy(q_woven[:].rearrange("p (q j) -> p q j", j=PACK), q_raw[:].rearrange("p j q -> p q j"))
-        rounded1 = place(pair_shape, BF16, "rounded1", IDENTITY, QUERIES_KIB)
-        gather_and_round(1, place([P, I], F32, "whole1", SHORT0_ROUNDED, 4)[:], 0, rounded1)
-        q_codes, q_scales = quantise_stationary(q_woven, "q", place([P, Q], U32, "q_codes", SHORT0_ROUNDED, 2))
+        picked_words = tile([P, I], U32, "picked_words", "book0", 4)
+        nc.vector.tensor_copy(picked_words, key_words.bitcast(U32).indirect(key_list[:]))
+        q_woven = tile([P, Q * PACK], BF16, "q_woven", "raw0")
+        nc.scalar.copy(q_woven.rearrange("p (q j) -> p q j", j=PACK), q_raw.rearrange("p (j q) -> p q j", j=PACK))
+        q_codes, q_scales = quantise_stationary(q_woven, "q")
         scores = ps.tile([P, I], F32, name="scores", tag="bank_e")
         nc.tensor.matmul_mx(
             out=scores[:],
-            lhsT=q_codes[:].bitcast(FP8X4),
-            lhsT_scale=q_scales[:],
+            lhsT=q_codes.bitcast(FP8X4),
+            lhsT_scale=q_scales,
             rhs=picked_words.bitcast(FP8X4),
-            rhs_scale=key_scales[:],
+            rhs_scale=key_scales,
             start=True,
             stop=True,
         )
-        size_bank = spread(size_col, "size_bank", "bank_f")
+        size_bank = spread(size_col, "size_bank", "bank_c")
+        prod1 = vector_gather(1, 0, vsc_low, "prod1", "q_raw")
+        raw1 = scalar_gather(1, HALF_I, HALF_I, "raw1", "q_raw")
+        rounded1 = tile(pair_shape, BF16, "rounded1")
+        scalar_round(rounded1, prod1, 0)
+        vector_round(rounded1, raw1, HALF_I)
+        raw2 = scalar_gather(2, 0, I, "raw2")
 
-        rounded2 = tile(pair_shape, BF16, "rounded2")
-        gather_and_round(2, place([P, I], F32, "whole2", IDENTITY, QUERIES_KIB + 1)[:], 0, rounded2)
-        woven0 = place(woven_shape(1), BF16, "woven0", SCORED)
-        weave_values(woven0, 0, bank0)
+        neg_max = tile([P, 1], F32, "neg_max")
+        nc.vector.tensor_reduce(neg_max, scores[:], AXIS.X, ALU.max, negate=True)
+        woven0 = woven_tile(1, "woven0", "picked_words")
+        weave(bank0, woven0[:, :, 0, :], nc.vector.tensor_copy)
         bank1 = turn(rounded1, "v1_bank", "bank_b")
-
-        neg_max = place([P, 1], F32, "neg_max", SCORED, 7)
-        nc.vector.tensor_reduce(neg_max[:], scores[:], AXIS.X, ALU.max, negate=True)
-        probs = tile(pair_shape, F32, "probs")
+        bank2 = ps.tile([P, PACK, P], F32, name="v2_bank", tag="bank_d")
+        for t in range(PACK):
+            nc.tensor.transpose(bank2[:, t, :], raw2[:, t:I:PACK], ident)
+        probs = tile(pair_shape, F32, "probs", "book2")
         row_sum = tile([P, 1], F32, "row_sum")
-        scores_by_pair = scores[:].rearrange("q (n u s) -> q u n s", u=PAIRS, s=PAIR)
-        nc.scalar.activation(probs[:], scores_by_pair, ACT.Exp, bias=neg_max[:], accum_out=row_sum[:])
-        bank2 = turn(rounded2, "v2_bank", "bank_e")
+        nc.scalar.activation(probs, by_pair(scores[:]), ACT.Exp, bias=neg_max, accum_out=row_sum)
 
         rounded3 = tile(pair_shape, BF16, "rounded3")
-        pieces = ((0, I - 2 * SHORT), (I - 2 * SHORT, SHORT), (LONG, SHORT))
-        for number, (first, count) in enumerate(pieces):
-            piece = place([P, count], F32, "piece3_%d" % number, SCORED, 2 + number)
-            gather_and_round(3, piece[:], first, rounded3)
-        bank3 = turn(rounded3, "v3_bank", "bank_d")
-        woven12 = place(woven_shape(2), BF16, "woven12", SCORED, 1 + len(pieces))
-        weave_values(woven12, 0, bank1)
-        weave_values(woven12, 1, bank2)
+        pieces = ((0, vsc_low), (HALF_I, vsc_high[:, 0:SHORT]), (I - SHORT, vsc_high[:, SHORT:HALF_I]))
+        for number, (first, factors) in enumerate(pieces):
+            scalar_round(rounded3, vector_gather(3, first, factors, "piece%d" % number, "picked_words"), first)
+        bank3 = turn(rounded3, "v3_bank", "bank_e")
 
-        inv_sum = tile([P, 1], F32, "inv_sum")
-        nc.vector.reciprocal(inv_sum[:], row_sum[:])
-        w_bank = ps.tile([P, PAIRS, Q], F32, name="w_bank", tag="bank_a")
+        inv_sum = tile([P, 1], F32, "inv_sum", "vsc_low")
+        nc.vector.reciprocal(inv_sum, row_sum)
+        v_codes = tile([P, HALVES, PACK, HALF_P], U32, "v_codes", "vsc_low")
+        v_scales = tile([P, HALVES, PACK, HALF_P], U8, "v_scales")
+        quantise_values(woven0, 0)
+        w_bank = ps.tile([P, PAIRS, Q], F32, name="w_bank", tag="bank_f")
         for u in range(PAIRS):
             weights = tile([P, P, PAIR], BF16, "weights%d" % u)
             nc.vector.scalar_tensor_tensor(
-                weights[:],
+                weights,
                 probs[:, u],
-                inv_sum[:],
+                inv_sum,
                 size_bank[:, PAIR * u : PAIR * (u + 1), :].rearrange("q s n -> q n s"),
                 ALU.mult,
                 ALU.mult,
             )
-            nc.tensor.transpose(w_bank[:, u, :], weights[:].rearrange("q n s -> q (n s)").bitcast(F32), ident[:])
-        woven3 = tile(woven_shape(1), BF16, "woven3")
-        weave_values(woven3, 0, bank3)
+            nc.tensor.transpose(w_bank[:, u, :], weights.rearrange("q n s -> q (n s)").bitcast(F32), ident)
 
-        v_codes = tile([P, HALVES, PACK, HALF_P], U32, "v_codes", "probs")
-        v_scales = tile([P, HALVES, PACK, HALF_P], U8, "v_scales")
-        quantise_values(woven0, 0)
-        quantise_values(woven12, 1)
-        w_woven = tile([P, Q * PACK], BF16, "w_woven")
-        nc.scalar.copy(
-            w_woven[:].bitcast(F32).rearrange("n (q u) -> n q u", u=PAIRS), w_bank[:].rearrange("n u q -> n q u")
+        woven1 = woven_tile(1, "woven1", "book3")
+        weave(bank1, woven1[:, :, 0, :])
+        woven3 = woven_tile(1, "woven3")
+        weave(bank3, woven3[:, :, 0, :])
+        w_woven = woven_tile(1, "w_woven")
+        weave(w_bank, w_woven[:, :, 0, :])
+        woven2 = woven_tile(1, "woven2", "probs")
+        nc.vector.tensor_tensor(
+            woven2.rearrange("n h j (r t) -> n (h j r) t", t=PACK),
+            bank2[:].rearrange("n t c -> n c t"),
+            vsc_kept.unsqueeze(1).to_broadcast([P, P, PACK]),
+            ALU.mult,
         )
-        quantise_values(woven3, 3)
-        w_codes, w_scales = quantise_stationary(w_woven, "w", tile([P, Q], U32, "w_codes"))
+        for j, woven in enumerate((woven1, woven2, woven3)):
+            quantise_values(woven, j + 1)
+        w_codes, w_scales = quantise_stationary(w_woven.rearrange("n h j r -> n (h j r)"), "w")
 
         for h in range(HALVES):
             sums = ps.tile([P, PACK, HALF_P], F32, name="sums%d" % h)
             nc.tensor.matmul_mx(
                 out=sums[:].rearrange("q j r -> q (j r)"),
-                lhsT=w_codes[:].bitcast(FP8X4),
-                lhsT_scale=w_scales[:],
+                lhsT=w_codes.bitcast(FP8X4),
+                lhsT_scale=w_scales,
                 rhs=v_codes[:, h, :, :].rearrange("n j r -> n (j r)").bitcast(FP8X4),
                 rhs_scale=v_scales[:, h, :, :].rearrange("n j r -> n (j r)"),
                 start=True,
@@ -229,6 +271,6 @@ def tile_attend_pqvalues_kernel(tc, query, keys_words, keys_scales, vbook, size,
             )
             result = tile([P, E // HALVES], F32, "result%d" % h)
             copy = (nc.vector.tensor_copy, nc.scalar.copy)[h]
-            copy(result[:].rearrange("q (r j) -> q r j", j=PACK), sums[:].rearrange("q j r -> q r j"))
+            copy(result.rearrange("q (r j) -> q r j", j=PACK), sums[:].rearrange("q j r -> q r j"))
             queue = (nc.sync, nc.scalar)[h]
-            queue.dma_start(out[:, h * (E // HALVES) : (h + 1) * (E // HALVES)], result[:])
+            queue.dma_start(out[:, h * (E // HALVES) : (h + 1) * (E // HALVES)], result)

@@ -91,9 +91,9 @@ def tile_attend_pqvalues_kernel(tc, query, keys_words, keys_scales, vbook, size,
             nc.sync.dma_start(
                 key_scales[r:P:QUADRANT, :].bitcast(I32), picked_bytes[BLOCK * r : P : QUADRANT, :].bitcast(I32)
             )
+        load_book("key_bytes")
         size_col = tile([P, PACK], F32, "size_col", "key_bytes")
         nc.sync.dma_start(size_col, size.rearrange("o (p t) -> p (o t)", t=PACK))
-        load_book("key_bytes")
         load_book("key_bytes")
 
         def spread(col, name, tag):

@@ -59,11 +59,11 @@ def tile_attend_pqvalues_kernel(tc, query, keys_words, keys_scales, vbook, size,
         ident = tile([P, P], F32, "ident")
 
         nc.vector.memset(key_bytes.bitcast(I32), 0)
-        key_scales = tile([P, I], U8, "key_scales")
-        nc.vector.memset(key_scales.bitcast(I32), 0)
         distance = tile([P, P], F32, "distance", room_kib=20)
         nc.gpsimd.iota(distance, [[1, P]], base=0, channel_multiplier=-1, allow_small_or_imprecise_dtypes=True)
-        nc.vector.tensor_scalar(ident, distance, 0.0, None, ALU.is_equal)
+        first_ident = tile([P, P], F32, "first_ident", room_kib=11)
+        for identity in (first_ident, ident):
+            nc.vector.tensor_scalar(identity, distance, 0.0, None, ALU.is_equal)
 
         book_rows = vbook.rearrange("(p j) c -> j p c", j=PACK)
         books = []
@@ -74,7 +74,7 @@ def tile_attend_pqvalues_kernel(tc, query, keys_words, keys_scales, vbook, size,
             books.append(book)
 
         load_book("", nc.scalar)
-        vsc_col = tile([P, PACK], F32, "vsc_col", room_kib=2)
+        vsc_col = tile([P, PACK], F32, "vsc_col")
         nc.sync.dma_start(vsc_col, vsc.rearrange("(p t) o -> p (t o)", t=PACK))
         nc.sync.dma_start(key_list[:], offs)
         nc.sync.dma_start(code_lists[:], offs2)
@@ -87,24 +87,24 @@ def tile_attend_pqvalues_kernel(tc, query, keys_words, keys_scales, vbook, size,
 
         picked_bytes = tile([P, I], U8, "picked_bytes", "distance")
         nc.vector.tensor_copy(picked_bytes, key_bytes.indirect(key_list[:]))
-        for r in range(PACK):
+        key_scales = tile([P, I], U8, "key_scales")
+        nc.vector.tensor_copy(key_scales.bitcast(I32), picked_bytes.bitcast(I32))
+        for r in range(1, PACK):
             nc.sync.dma_start(
                 key_scales[r:P:QUADRANT, :].bitcast(I32), picked_bytes[BLOCK * r : P : QUADRANT, :].bitcast(I32)
             )
-        load_book("key_bytes")
-        size_col = tile([P, PACK], F32, "size_col", "key_bytes")
-        nc.sync.dma_start(size_col, size.rearrange("o (p t) -> p (o t)", t=PACK))
-        load_book("key_bytes")
 
-        def spread(col, name, tag):
+        def spread(col, name, tag, identity):
             bank = ps.tile([P, PACK, P], F32, name=name, tag=tag)
             for t in range(PACK):
-                nc.tensor.transpose(bank[:, t, :], col[:, t : t + 1].to_broadcast([P, P]), ident)
+                nc.tensor.transpose(bank[:, t, :], col[:, t : t + 1].to_broadcast([P, P]), identity)
             return bank
 
-        vsc_kept = tile([P, PACK], F32, "vsc_kept")
-        nc.gpsimd.tensor_copy(vsc_kept, vsc_col)
-        vsc_bank = spread(vsc_col, "vsc_bank", "bank_a")
+        vsc_bank = spread(vsc_col, "vsc_bank", "bank_a", first_ident)
+        load_book("first_ident")
+        size_col = tile([P, PACK], F32, "size_col", "first_ident")
+        nc.sync.dma_start(size_col, size.rearrange("o (p t) -> p (o t)", t=PACK))
+        load_book("first_ident")
 
 
         def vsc_half(first, name, room_kib=0):
@@ -177,7 +177,7 @@ def tile_attend_pqvalues_kernel(tc, query, keys_words, keys_scales, vbook, size,
         pair_shape = [P, PAIRS, P, PAIR]
 
         rounded0 = tile(pair_shape, BF16, "rounded0", "key_bytes")
-        raw0 = scalar_gather(0, 0, I, "raw0", "vsc_col")
+        raw0 = scalar_gather(0, 0, I, "raw0", "first_ident")
         vsc_high = vsc_half(HALF_I, "vsc_high")
         vector_round(rounded0, raw0, 0)
         bank0 = turn(rounded0, "v0_bank", "bank_b")
@@ -197,7 +197,7 @@ def tile_attend_pqvalues_kernel(tc, query, keys_words, keys_scales, vbook, size,
             start=True,
             stop=True,
         )
-        size_bank = spread(size_col, "size_bank", "bank_c")
+        size_bank = spread(size_col, "size_bank", "bank_c", ident)
         prod1 = vector_gather(1, 0, vsc_low, "prod1", "q_raw")
         raw1 = scalar_gather(1, HALF_I, HALF_I, "raw1", "q_raw")
         rounded1 = tile(pair_shape, BF16, "rounded1")
@@ -251,7 +251,7 @@ def tile_attend_pqvalues_kernel(tc, query, keys_words, keys_scales, vbook, size,
         nc.vector.tensor_tensor(
             woven2.rearrange("n h j (r t) -> n (h j r) t", t=PACK),
             bank2[:].rearrange("n t c -> n c t"),
-            vsc_kept.unsqueeze(1).to_broadcast([P, P, PACK]),
+            vsc_col.unsqueeze(1).to_broadcast([P, P, PACK]),
             ALU.mult,
         )
         for j, woven in enumerate((woven1, woven2, woven3)):

@@ -62,8 +62,8 @@ def tile_attend_pqvalues_kernel(tc, query, keys_words, keys_scales, vbook, size,
         distance = tile([P, P], F32, "distance", room_kib=20)
         nc.gpsimd.iota(distance, [[1, P]], base=0, channel_multiplier=-1, allow_small_or_imprecise_dtypes=True)
         first_ident = tile([P, P], F32, "first_ident", room_kib=11)
-        for identity in (first_ident, ident):
-            nc.vector.tensor_scalar(identity, distance, 0.0, None, ALU.is_equal)
+        nc.vector.tensor_scalar(first_ident, distance, 0.0, None, ALU.is_equal)
+        nc.vector.tensor_copy(ident, first_ident)
 
         book_rows = vbook.rearrange("(p j) c -> j p c", j=PACK)
         books = []
@@ -85,7 +85,7 @@ def tile_attend_pqvalues_kernel(tc, query, keys_words, keys_scales, vbook, size,
         nc.sync.dma_start(q_raw.rearrange("p (j q) -> p j q", j=PACK), query.rearrange("(p j) q -> p j q", j=PACK))
         load_book("distance")
 
-        picked_bytes = tile([P, I], U8, "picked_bytes", "distance")
+        picked_bytes = tile([P, I], U8, "picked_bytes", "distance", 1)
         nc.vector.tensor_copy(picked_bytes, key_bytes.indirect(key_list[:]))
         key_scales = tile([P, I], U8, "key_scales")
         nc.vector.tensor_copy(key_scales.bitcast(I32), picked_bytes.bitcast(I32))
@@ -107,13 +107,13 @@ def tile_attend_pqvalues_kernel(tc, query, keys_words, keys_scales, vbook, size,
         load_book("first_ident")
 
 
-        def vsc_half(first, name, room_kib=0):
-            row = tile([P, HALF_I], F32, name, "", room_kib)
-            rows = slice(first // PACK, (first + HALF_I) // PACK)
+        def vsc_part(first, count, name, room_kib=0):
+            row = tile([P, count], F32, name, "", room_kib)
+            rows = slice(first // PACK, (first + count) // PACK)
             nc.scalar.copy(row.rearrange("p (n t) -> p n t", t=PACK), vsc_bank[:, :, rows].rearrange("p t n -> p n t"))
             return row
 
-        vsc_low = vsc_half(0, "vsc_low", 4)
+        vsc_low = vsc_part(0, I - SHORT, "vsc_low", 4)
 
         def by_pair(columns):
             return columns.rearrange("p (n u s) -> p u n s", u=PAIRS, s=PAIR)
@@ -177,9 +177,11 @@ def tile_attend_pqvalues_kernel(tc, query, keys_words, keys_scales, vbook, size,
         pair_shape = [P, PAIRS, P, PAIR]
 
         rounded0 = tile(pair_shape, BF16, "rounded0", "key_bytes")
-        raw0 = scalar_gather(0, 0, I, "raw0", "first_ident")
-        vsc_high = vsc_half(HALF_I, "vsc_high")
-        vector_round(rounded0, raw0, 0)
+        raw0 = scalar_gather(0, HALF_I, HALF_I, "raw0", "first_ident", 2)
+        prod0 = vector_gather(0, 0, vsc_low[:, 0:HALF_I], "prod0", "key_bytes")
+        scalar_round(rounded0, prod0, 0)
+        vsc_high = vsc_part(I - SHORT, SHORT, "vsc_high")
+        vector_round(rounded0, raw0, HALF_I)
         bank0 = turn(rounded0, "v0_bank", "bank_b")
 
         picked_words = tile([P, I], U32, "picked_words", "book0", 4)
@@ -198,17 +200,17 @@ def tile_attend_pqvalues_kernel(tc, query, keys_words, keys_scales, vbook, size,
             stop=True,
         )
         size_bank = spread(size_col, "size_bank", "bank_c", ident)
-        prod1 = vector_gather(1, 0, vsc_low, "prod1", "q_raw")
-        raw1 = scalar_gather(1, HALF_I, HALF_I, "raw1", "q_raw")
-        rounded1 = tile(pair_shape, BF16, "rounded1")
+        woven0 = woven_tile(1, "woven0", "q_raw")
+        weave(bank0, woven0[:, :, 0, :])
+        prod1 = vector_gather(1, 0, vsc_low[:, 0:HALF_I], "prod1", "q_raw")
+        raw1 = scalar_gather(1, HALF_I, HALF_I, "raw1", "raw0")
+        rounded1 = tile(pair_shape, BF16, "rounded1", "picked_bytes")
         scalar_round(rounded1, prod1, 0)
         vector_round(rounded1, raw1, HALF_I)
         raw2 = scalar_gather(2, 0, I, "raw2")
 
         neg_max = tile([P, 1], F32, "neg_max")
         nc.vector.tensor_reduce(neg_max, scores[:], AXIS.X, ALU.max, negate=True)
-        woven0 = woven_tile(1, "woven0", "picked_words")
-        weave(bank0, woven0[:, :, 0, :], nc.vector.tensor_copy)
         bank1 = turn(rounded1, "v1_bank", "bank_b")
         bank2 = ps.tile([P, PACK, P], F32, name="v2_bank", tag="bank_d")
         for t in range(PACK):
@@ -218,7 +220,7 @@ def tile_attend_pqvalues_kernel(tc, query, keys_words, keys_scales, vbook, size,
         nc.scalar.activation(probs, by_pair(scores[:]), ACT.Exp, bias=neg_max, accum_out=row_sum)
 
         rounded3 = tile(pair_shape, BF16, "rounded3")
-        pieces = ((0, vsc_low), (HALF_I, vsc_high[:, 0:SHORT]), (I - SHORT, vsc_high[:, SHORT:HALF_I]))
+        pieces = ((0, vsc_low), (I - SHORT, vsc_high))
         for number, (first, factors) in enumerate(pieces):
             scalar_round(rounded3, vector_gather(3, first, factors, "piece%d" % number, "picked_words"), first)
         bank3 = turn(rounded3, "v3_bank", "bank_e")

@@ -28,6 +28,7 @@ HALF_P = P // HALVES
 HALF_I = I // 2
 SHORT = 128
 KIB = 1024
+ROW_OF_BOOK = (0, 2, 1, 3)
 
 
 def tile_attend_pqvalues_kernel(tc, query, keys_words, keys_scales, vbook, size, vsc, offs, offs2, out):
@@ -55,34 +56,34 @@ def tile_attend_pqvalues_kernel(tc, query, keys_words, keys_scales, vbook, size,
 
         key_list = sb.tile([P, I // GROUP], U16, name="key_list")
         code_lists = sb.tile([P, I // GROUP], U16, name="code_lists")
-        key_bytes = tile([P, T], U8, "key_bytes", room_kib=10)
+        key_bytes = tile([P, T], U8, "key_bytes", room_kib=4)
         ident = tile([P, P], F32, "ident")
 
         nc.vector.memset(key_bytes.bitcast(I32), 0)
         distance = tile([P, P], F32, "distance", room_kib=20)
         nc.gpsimd.iota(distance, [[1, P]], base=0, channel_multiplier=-1, allow_small_or_imprecise_dtypes=True)
-        first_ident = tile([P, P], F32, "first_ident", room_kib=11)
+        first_ident = tile([P, P], F32, "first_ident", room_kib=12)
         nc.vector.tensor_scalar(first_ident, distance, 0.0, None, ALU.is_equal)
         nc.vector.tensor_copy(ident, first_ident)
 
         book_rows = vbook.rearrange("(p j) c -> j p c", j=PACK)
         books = []
 
-        def load_book(behind, queue=nc.sync):
+        def load_book(behind):
             book = tile([P, C], F32, "book%d" % len(books), behind)
-            queue.dma_start(book, book_rows[len(books)])
+            nc.sync.dma_start(book, book_rows[ROW_OF_BOOK[len(books)]])
             books.append(book)
 
-        load_book("", nc.scalar)
+        q_raw = tile([P, PACK * Q], F32, "q_raw")
+        nc.scalar.dma_start(q_raw.rearrange("p (j q) -> p j q", j=PACK), query.rearrange("(p j) q -> p j q", j=PACK))
         vsc_col = tile([P, PACK], F32, "vsc_col")
         nc.sync.dma_start(vsc_col, vsc.rearrange("(p t) o -> p (t o)", t=PACK))
         nc.sync.dma_start(key_list[:], offs)
         nc.sync.dma_start(code_lists[:], offs2)
         nc.sync.dma_start(key_bytes[0:P:BLOCK, :].bitcast(I32), keys_scales[0].bitcast(I32))
+        load_book("distance")
         key_words = tile([P, T], I32, "key_words", "distance")
         nc.sync.dma_start(key_words, keys_words[0].rearrange("p n t -> p (n t)").bitcast(I32))
-        q_raw = tile([P, PACK * Q], F32, "q_raw", "distance")
-        nc.sync.dma_start(q_raw.rearrange("p (j q) -> p j q", j=PACK), query.rearrange("(p j) q -> p j q", j=PACK))
         load_book("distance")
 
         picked_bytes = tile([P, I], U8, "picked_bytes", "distance", 1)
@@ -106,14 +107,12 @@ def tile_attend_pqvalues_kernel(tc, query, keys_words, keys_scales, vbook, size,
         nc.sync.dma_start(size_col, size.rearrange("o (p t) -> p (o t)", t=PACK))
         load_book("first_ident")
 
-
-        def vsc_part(first, count, name, room_kib=0):
-            row = tile([P, count], F32, name, "", room_kib)
-            rows = slice(first // PACK, (first + count) // PACK)
-            nc.scalar.copy(row.rearrange("p (n t) -> p n t", t=PACK), vsc_bank[:, :, rows].rearrange("p t n -> p n t"))
-            return row
-
-        vsc_low = vsc_part(0, I - SHORT, "vsc_low", 4)
+        q_woven = tile([P, Q * PACK], BF16, "q_woven")
+        nc.scalar.copy(q_woven.rearrange("p (q j) -> p q j", j=PACK), q_raw.rearrange("p (j q) -> p q j", j=PACK))
+        vsc_low = tile([P, HALF_I], F32, "vsc_low", "", 3)
+        nc.scalar.copy(
+            vsc_low.rearrange("p (n t) -> p n t", t=PACK), vsc_bank[:, :, 0 : HALF_I // PACK].rearrange("p t n -> p n t")
+        )
 
         def by_pair(columns):
             return columns.rearrange("p (n u s) -> p u n s", u=PAIRS, s=PAIR)
@@ -135,8 +134,8 @@ def tile_attend_pqvalues_kernel(tc, query, keys_words, keys_scales, vbook, size,
             nc.scalar.activation(raw, listed(j, first, count), ACT.Copy)
             return raw
 
-        def scalar_round(rounded, prod, first):
-            nc.scalar.copy(slots(rounded, first, prod.shape[1]), by_pair(prod))
+        def plain_round(rounded, prod, first, copy=nc.scalar.copy):
+            copy(slots(rounded, first, prod.shape[1]), by_pair(prod))
 
         def vector_round(rounded, raw, first):
             count = raw.shape[1]
@@ -156,39 +155,44 @@ def tile_attend_pqvalues_kernel(tc, query, keys_words, keys_scales, vbook, size,
                 bank[:].rearrange("n u (h r) -> n h r u", h=HALVES),
             )
 
-        def woven_tile(count, name, behind=""):
-            return tile([P, HALVES, count, HALF_P * PACK], BF16, name, behind)
-
-        def quantise_values(woven, first):
-            these = slice(first, first + woven.shape[2])
-            for h in range(HALVES):
-                nc.vector.quantize_mx(
-                    out=v_codes[:, h, these, :].rearrange("n j r -> n (j r)").bitcast(FP8X4),
-                    scales=v_scales[:, h, these, :].rearrange("n j r -> n (j r)"),
-                    in_=woven[:, h, :, :].rearrange("n j r -> n (j r)"),
-                )
-
-        def quantise_stationary(woven, name, behind=""):
-            codes = tile([P, Q], U32, name + "_codes", behind)
-            scales = tile([P, Q], U8, name + "_scales")
+        def quantise(woven, name, behind=""):
+            codes = tile([P, P], U32, name + "_codes", behind)
+            scales = tile([P, P], U8, name + "_scales")
             nc.vector.quantize_mx(out=codes.bitcast(FP8X4), scales=scales, in_=woven)
             return codes, scales
 
+        def by_half(woven):
+            return woven.rearrange("n (h r) -> n h r", h=HALVES)
+
         pair_shape = [P, PAIRS, P, PAIR]
 
+        def value_tiles(name, behind):
+            codes = tile([P, HALVES, PAIR, HALF_P], U32, name + "_codes", behind)
+            scales = tile([P, HALVES, PAIR, HALF_P], U8, name + "_scales")
+            return codes, scales
+
+        def quantise_book(pair, place, woven):
+            codes, scales = pair
+            for h in range(HALVES):
+                nc.vector.quantize_mx(
+                    out=codes[:, h, place, :].bitcast(FP8X4), scales=scales[:, h, place, :], in_=by_half(woven)[:, h, :]
+                )
+
+        def woven_from(bank, name, behind=""):
+            woven = tile([P, P * PACK], BF16, name, behind)
+            weave(bank, by_half(woven))
+            return woven
+
+        raw0 = scalar_gather(0, HALF_I, HALF_I, "raw0", "first_ident")
+        prod0 = vector_gather(0, 0, vsc_low, "prod0", "key_bytes")
         rounded0 = tile(pair_shape, BF16, "rounded0", "key_bytes")
-        raw0 = scalar_gather(0, HALF_I, HALF_I, "raw0", "first_ident", 2)
-        prod0 = vector_gather(0, 0, vsc_low[:, 0:HALF_I], "prod0", "key_bytes")
-        scalar_round(rounded0, prod0, 0)
-        vsc_high = vsc_part(I - SHORT, SHORT, "vsc_high")
+        plain_round(rounded0, prod0, 0)
         vector_round(rounded0, raw0, HALF_I)
         bank0 = turn(rounded0, "v0_bank", "bank_b")
+        q_codes, q_scales = quantise(q_woven, "q", "key_bytes")
 
-        picked_words = tile([P, I], U32, "picked_words", "book0", 4)
+        picked_words = tile([P, I], U32, "picked_words", "book0")
         nc.vector.tensor_copy(picked_words, key_words.bitcast(U32).indirect(key_list[:]))
-        q_woven = tile([P, Q * PACK], BF16, "q_woven", "raw0")
-        nc.scalar.copy(q_woven.rearrange("p (q j) -> p q j", j=PACK), q_raw.rearrange("p (j q) -> p q j", j=PACK))
-        q_codes, q_scales = quantise_stationary(q_woven, "q")
         scores = ps.tile([P, I], F32, name="scores", tag="bank_e")
         nc.tensor.matmul_mx(
             out=scores[:],
@@ -199,80 +203,80 @@ def tile_attend_pqvalues_kernel(tc, query, keys_words, keys_scales, vbook, size,
             start=True,
             stop=True,
         )
-        size_bank = spread(size_col, "size_bank", "bank_c", ident)
-        woven0 = woven_tile(1, "woven0", "q_raw")
-        weave(bank0, woven0[:, :, 0, :])
-        prod1 = vector_gather(1, 0, vsc_low[:, 0:HALF_I], "prod1", "q_raw")
+        woven0 = woven_from(bank0, "woven0")
+        prod1 = vector_gather(1, 0, vsc_low, "prod1", "key_words")
         raw1 = scalar_gather(1, HALF_I, HALF_I, "raw1", "raw0")
+        even = value_tiles("even", "key_words")
+        quantise_book(even, 0, woven0)
         rounded1 = tile(pair_shape, BF16, "rounded1", "picked_bytes")
-        scalar_round(rounded1, prod1, 0)
         vector_round(rounded1, raw1, HALF_I)
-        raw2 = scalar_gather(2, 0, I, "raw2")
-
         neg_max = tile([P, 1], F32, "neg_max")
         nc.vector.tensor_reduce(neg_max, scores[:], AXIS.X, ALU.max, negate=True)
+        plain_round(rounded1, prod1, 0, nc.vector.tensor_copy)
+        size_bank = spread(size_col, "size_bank", "bank_c", ident)
         bank1 = turn(rounded1, "v1_bank", "bank_b")
+
+        raw2 = scalar_gather(2, 0, I, "raw2")
         bank2 = ps.tile([P, PACK, P], F32, name="v2_bank", tag="bank_d")
         for t in range(PACK):
             nc.tensor.transpose(bank2[:, t, :], raw2[:, t:I:PACK], ident)
         probs = tile(pair_shape, F32, "probs", "book2")
-        row_sum = tile([P, 1], F32, "row_sum")
+        row_sum = tile([P, 1], F32, "row_sum", "", 1)
         nc.scalar.activation(probs, by_pair(scores[:]), ACT.Exp, bias=neg_max, accum_out=row_sum)
-
-        rounded3 = tile(pair_shape, BF16, "rounded3")
-        pieces = ((0, vsc_low), (I - SHORT, vsc_high))
-        for number, (first, factors) in enumerate(pieces):
-            scalar_round(rounded3, vector_gather(3, first, factors, "piece%d" % number, "picked_words"), first)
-        bank3 = turn(rounded3, "v3_bank", "bank_e")
-
+        raw3 = scalar_gather(3, HALF_I, HALF_I, "raw3")
+        prod3 = vector_gather(3, 0, vsc_low, "prod3")
         inv_sum = tile([P, 1], F32, "inv_sum", "vsc_low")
         nc.vector.reciprocal(inv_sum, row_sum)
-        v_codes = tile([P, HALVES, PACK, HALF_P], U32, "v_codes", "vsc_low")
-        v_scales = tile([P, HALVES, PACK, HALF_P], U8, "v_scales")
-        quantise_values(woven0, 0)
+        rounded3 = tile(pair_shape, BF16, "rounded3", "row_sum")
+        plain_round(rounded3, prod3, 0)
+        woven1 = woven_from(bank1, "woven1", "book3")
+
         w_bank = ps.tile([P, PAIRS, Q], F32, name="w_bank", tag="bank_f")
         for u in range(PAIRS):
-            weights = tile([P, P, PAIR], BF16, "weights%d" % u)
+            weights = tile([P, P * PAIR], BF16, "weights%d" % u)
             nc.vector.scalar_tensor_tensor(
-                weights,
+                weights.rearrange("q (n s) -> q n s", s=PAIR),
                 probs[:, u],
                 inv_sum,
                 size_bank[:, PAIR * u : PAIR * (u + 1), :].rearrange("q s n -> q n s"),
                 ALU.mult,
                 ALU.mult,
             )
-            nc.tensor.transpose(w_bank[:, u, :], weights.rearrange("q n s -> q (n s)").bitcast(F32), ident)
+            nc.tensor.transpose(w_bank[:, u, :], weights.bitcast(F32), ident)
+        vector_round(rounded3, raw3, HALF_I)
+        bank3 = turn(rounded3, "v3_bank", "bank_e")
 
-        woven1 = woven_tile(1, "woven1", "book3")
-        weave(bank1, woven1[:, :, 0, :])
-        woven3 = woven_tile(1, "woven3")
-        weave(bank3, woven3[:, :, 0, :])
-        w_woven = woven_tile(1, "w_woven")
-        weave(w_bank, w_woven[:, :, 0, :])
-        woven2 = woven_tile(1, "woven2", "probs")
+        w_woven = woven_from(w_bank, "w_woven")
+        woven3 = woven_from(bank3, "woven3")
+        woven2 = tile([P, P * PACK], BF16, "woven2", "probs")
         nc.vector.tensor_tensor(
-            woven2.rearrange("n h j (r t) -> n (h j r) t", t=PACK),
+            woven2.rearrange("n (c t) -> n c t", t=PACK),
             bank2[:].rearrange("n t c -> n c t"),
             vsc_col.unsqueeze(1).to_broadcast([P, P, PACK]),
             ALU.mult,
         )
-        for j, woven in enumerate((woven1, woven2, woven3)):
-            quantise_values(woven, j + 1)
-        w_codes, w_scales = quantise_stationary(w_woven.rearrange("n h j r -> n (h j r)"), "w")
+        odd = value_tiles("odd", "probs")
+        quantise_book(odd, 0, woven1)
+        quantise_book(even, 1, woven2)
+        w_codes, w_scales = quantise(w_woven, "w")
+        quantise_book(odd, 1, woven3)
 
+        sums = [ps.tile([P, PACK, HALF_P], F32, name="sums%d" % h) for h in range(HALVES)]
+        for number, (codes, scales) in enumerate((even, odd)):
+            these = slice(number * PAIR, (number + 1) * PAIR)
+            for h in range(HALVES):
+                nc.tensor.matmul_mx(
+                    out=sums[h][:, these, :].rearrange("q j r -> q (j r)"),
+                    lhsT=w_codes.bitcast(FP8X4),
+                    lhsT_scale=w_scales,
+                    rhs=codes[:, h].rearrange("n j r -> n (j r)").bitcast(FP8X4),
+                    rhs_scale=scales[:, h].rearrange("n j r -> n (j r)"),
+                    start=True,
+                    stop=True,
+                )
         for h in range(HALVES):
-            sums = ps.tile([P, PACK, HALF_P], F32, name="sums%d" % h)
-            nc.tensor.matmul_mx(
-                out=sums[:].rearrange("q j r -> q (j r)"),
-                lhsT=w_codes.bitcast(FP8X4),
-                lhsT_scale=w_scales,
-                rhs=v_codes[:, h, :, :].rearrange("n j r -> n (j r)").bitcast(FP8X4),
-                rhs_scale=v_scales[:, h, :, :].rearrange("n j r -> n (j r)"),
-                start=True,
-                stop=True,
-            )
             result = tile([P, E // HALVES], F32, "result%d" % h)
             copy = (nc.vector.tensor_copy, nc.scalar.copy)[h]
-            copy(result.rearrange("q (r j) -> q r j", j=PACK), sums[:].rearrange("q j r -> q r j"))
+            copy(result.rearrange("q (r j) -> q r j", j=PACK), sums[h][:].rearrange("q j r -> q r j"))
             queue = (nc.sync, nc.scalar)[h]
             queue.dma_start(out[:, h * (E // HALVES) : (h + 1) * (E // HALVES)], result)

@@ -96,9 +96,9 @@ def tile_attend_pqvalues_kernel(tc, query, keys_words, keys_scales, vbook, size,
             )
 
         def spread(col, name, tag, identity):
-            bank = ps.tile([P, PACK, P], F32, name=name, tag=tag)
+            bank = ps.tile([P, PAIRS, P, PAIR], F32, name=name, tag=tag)
             for t in range(PACK):
-                nc.tensor.transpose(bank[:, t, :], col[:, t : t + 1].to_broadcast([P, P]), identity)
+                nc.tensor.transpose(bank[:, t // PAIR, :, t % PAIR], col[:, t : t + 1].to_broadcast([P, P]), identity)
             return bank
 
         vsc_bank = spread(vsc_col, "vsc_bank", "bank_a", first_ident)
@@ -111,7 +111,8 @@ def tile_attend_pqvalues_kernel(tc, query, keys_words, keys_scales, vbook, size,
         nc.scalar.copy(q_woven.rearrange("p (q j) -> p q j", j=PACK), q_raw.rearrange("p (j q) -> p q j", j=PACK))
         vsc_low = tile([P, HALF_I], F32, "vsc_low", "", 3)
         nc.scalar.copy(
-            vsc_low.rearrange("p (n t) -> p n t", t=PACK), vsc_bank[:, :, 0 : HALF_I // PACK].rearrange("p t n -> p n t")
+            vsc_low.rearrange("p (n u s) -> p n u s", u=PAIRS, s=PAIR),
+            vsc_bank[:, :, 0 : HALF_I // PACK, :].rearrange("p u n s -> p n u s"),
         )
 
         def by_pair(columns):
@@ -139,8 +140,7 @@ def tile_attend_pqvalues_kernel(tc, query, keys_words, keys_scales, vbook, size,
 
         def vector_round(rounded, raw, first):
             count = raw.shape[1]
-            factors = vsc_bank[:].rearrange("p (u s) n -> p u n s", s=PAIR)
-            nc.vector.tensor_tensor(slots(rounded, first, count), by_pair(raw), slots(factors, first, count), ALU.mult)
+            nc.vector.tensor_tensor(slots(rounded, first, count), by_pair(raw), slots(vsc_bank, first, count), ALU.mult)
 
         def turn(rounded, name, tag):
             bank = ps.tile([P, PAIRS, P], F32, name=name, tag=tag)
@@ -217,9 +217,9 @@ def tile_attend_pqvalues_kernel(tc, query, keys_words, keys_scales, vbook, size,
         bank1 = turn(rounded1, "v1_bank", "bank_b")
 
         raw2 = scalar_gather(2, 0, I, "raw2")
-        bank2 = ps.tile([P, PACK, P], F32, name="v2_bank", tag="bank_d")
+        bank2 = ps.tile([P, P, PACK], F32, name="v2_bank", tag="bank_d")
         for t in range(PACK):
-            nc.tensor.transpose(bank2[:, t, :], raw2[:, t:I:PACK], ident)
+            nc.tensor.transpose(bank2[:, :, t], raw2[:, t:I:PACK], ident)
         probs = tile(pair_shape, F32, "probs", "book2")
         row_sum = tile([P, 1], F32, "row_sum", "", 1)
         nc.scalar.activation(probs, by_pair(scores[:]), ACT.Exp, bias=neg_max, accum_out=row_sum)
@@ -238,7 +238,7 @@ def tile_attend_pqvalues_kernel(tc, query, keys_words, keys_scales, vbook, size,
                 weights.rearrange("q (n s) -> q n s", s=PAIR),
                 probs[:, u],
                 inv_sum,
-                size_bank[:, PAIR * u : PAIR * (u + 1), :].rearrange("q s n -> q n s"),
+                size_bank[:, u],
                 ALU.mult,
                 ALU.mult,
             )
@@ -251,7 +251,7 @@ def tile_attend_pqvalues_kernel(tc, query, keys_words, keys_scales, vbook, size,
         woven2 = tile([P, P * PACK], BF16, "woven2", "probs")
         nc.vector.tensor_tensor(
             woven2.rearrange("n (c t) -> n c t", t=PACK),
-            bank2[:].rearrange("n t c -> n c t"),
+            bank2[:],
             vsc_col.unsqueeze(1).to_broadcast([P, P, PACK]),
             ALU.mult,
         )

@@ -206,8 +206,6 @@ def tile_attend_pqvalues_kernel(tc, query, keys_words, keys_scales, vbook, size,
         woven0 = woven_from(bank0, "woven0")
         prod1 = vector_gather(1, 0, vsc_low, "prod1", "key_words")
         raw1 = scalar_gather(1, HALF_I, HALF_I, "raw1", "raw0")
-        even = value_tiles("even", "key_words")
-        quantise_book(even, 0, woven0)
         rounded1 = tile(pair_shape, BF16, "rounded1", "picked_bytes")
         vector_round(rounded1, raw1, HALF_I)
         neg_max = tile([P, 1], F32, "neg_max")
@@ -227,6 +225,8 @@ def tile_attend_pqvalues_kernel(tc, query, keys_words, keys_scales, vbook, size,
         prod3 = vector_gather(3, 0, vsc_low, "prod3")
         inv_sum = tile([P, 1], F32, "inv_sum", "vsc_low")
         nc.vector.reciprocal(inv_sum, row_sum)
+        even = value_tiles("even", "vsc_low")
+        quantise_book(even, 0, woven0)
         rounded3 = tile(pair_shape, BF16, "rounded3", "row_sum")
         plain_round(rounded3, prod3, 0)
         woven1 = woven_from(bank1, "woven1", "book3")
@@ -277,6 +277,9 @@ def tile_attend_pqvalues_kernel(tc, query, keys_words, keys_scales, vbook, size,
         for h in range(HALVES):
             result = tile([P, E // HALVES], F32, "result%d" % h)
             copy = (nc.vector.tensor_copy, nc.scalar.copy)[h]
-            copy(result.rearrange("q (r j) -> q r j", j=PACK), sums[h][:].rearrange("q j r -> q r j"))
+            copy(
+                result.rearrange("q (c i j) -> q c j i", i=PAIR, j=PACK),
+                sums[h][:].rearrange("q j (c i) -> q c j i", i=PAIR),
+            )
             queue = (nc.sync, nc.scalar)[h]
             queue.dma_start(out[:, h * (E // HALVES) : (h + 1) * (E // HALVES)], result)

@@ -138,9 +138,14 @@ def tile_attend_pqvalues_kernel(tc, query, keys_words, keys_scales, vbook, size,
         def plain_round(rounded, prod, first, copy=nc.scalar.copy):
             copy(slots(rounded, first, prod.shape[1]), by_pair(prod))
 
-        def vector_round(rounded, raw, first):
+        def vector_round(rounded, raw, first, pairs=slice(0, PAIRS)):
             count = raw.shape[1]
-            nc.vector.tensor_tensor(slots(rounded, first, count), by_pair(raw), slots(vsc_bank, first, count), ALU.mult)
+            nc.vector.tensor_tensor(
+                slots(rounded, first, count)[:, pairs],
+                by_pair(raw)[:, pairs],
+                slots(vsc_bank, first, count)[:, pairs],
+                ALU.mult,
+            )
 
         def turn(rounded, name, tag):
             bank = ps.tile([P, PAIRS, P], F32, name=name, tag=tag)
@@ -243,11 +248,17 @@ def tile_attend_pqvalues_kernel(tc, query, keys_words, keys_scales, vbook, size,
                 ALU.mult,
             )
             nc.tensor.transpose(w_bank[:, u, :], weights.bitcast(F32), ident)
-        vector_round(rounded3, raw3, HALF_I)
+        for u in range(PAIRS):
+            vector_round(rounded3, raw3, HALF_I, slice(u, u + 1))
         bank3 = turn(rounded3, "v3_bank", "bank_e")
 
         w_woven = woven_from(w_bank, "w_woven")
-        woven3 = woven_from(bank3, "woven3")
+        woven3 = tile([P, P * PACK], BF16, "woven3")
+        for h in range(HALVES):
+            nc.scalar.copy(
+                by_half(woven3)[:, h, :].bitcast(F32).rearrange("n (r u) -> n r u", u=PAIRS),
+                bank3[:, :, h * HALF_P : (h + 1) * HALF_P].rearrange("n u r -> n r u"),
+            )
         woven2 = tile([P, P * PACK], BF16, "woven2", "probs")
         nc.vector.tensor_tensor(
             woven2.rearrange("n (c t) -> n c t", t=PACK),
@@ -256,9 +267,9 @@ def tile_attend_pqvalues_kernel(tc, query, keys_words, keys_scales, vbook, size,
             ALU.mult,
         )
         odd = value_tiles("odd", "probs")
-        quantise_book(odd, 0, woven1)
-        quantise_book(even, 1, woven2)
         w_codes, w_scales = quantise(w_woven, "w")
+        quantise_book(even, 1, woven2)
+        quantise_book(odd, 0, woven1)
         quantise_book(odd, 1, woven3)
 
         sums = [ps.tile([P, PACK, HALF_P], F32, name="sums%d" % h) for h in range(HALVES)]

@@ -80,6 +80,8 @@ def tile_attend_pqvalues_kernel(tc, query, keys_words, keys_scales, vbook, size,
         nc.sync.dma_start(vsc_col, vsc.rearrange("(p t) o -> p (t o)", t=PACK))
         nc.sync.dma_start(key_list[:], offs)
         nc.sync.dma_start(code_lists[:], offs2)
+        size_col = tile([P, PACK], F32, "size_col")
+        nc.sync.dma_start(size_col, size.rearrange("o (p t) -> p (o t)", t=PACK))
         nc.sync.dma_start(key_bytes[0:P:BLOCK, :].bitcast(I32), keys_scales[0].bitcast(I32))
         load_book("distance")
         key_words = tile([P, T], I32, "key_words", "distance")
@@ -103,8 +105,6 @@ def tile_attend_pqvalues_kernel(tc, query, keys_words, keys_scales, vbook, size,
 
         vsc_bank = spread(vsc_col, "vsc_bank", "bank_a", first_ident)
         load_book("first_ident")
-        size_col = tile([P, PACK], F32, "size_col", "first_ident")
-        nc.sync.dma_start(size_col, size.rearrange("o (p t) -> p (o t)", t=PACK))
         load_book("first_ident")
 
         q_woven = tile([P, Q * PACK], BF16, "q_woven")

@@ -148,17 +148,14 @@ def tile_attend_pqvalues_kernel(tc, query, keys_words, keys_scales, vbook, size,
             )
 
         def turn(rounded, name, tag):
-            bank = ps.tile([P, PAIRS, P], F32, name=name, tag=tag)
+            bank = ps.tile([P, P, PAIRS], F32, name=name, tag=tag)
             for u in range(PAIRS):
                 words = rounded[:, u].rearrange("p n s -> p (n s)").bitcast(F32)
-                nc.tensor.transpose(bank[:, u, :], words, ident)
+                nc.tensor.transpose(bank[:, :, u], words, ident)
             return bank
 
         def weave(bank, woven, copy=nc.scalar.copy):
-            copy(
-                woven.bitcast(F32).rearrange("n h (r u) -> n h r u", u=PAIRS),
-                bank[:].rearrange("n u (h r) -> n h r u", h=HALVES),
-            )
+            copy(woven.bitcast(F32), bank[:].rearrange("n p u -> n (p u)"))
 
         def quantise(woven, name, behind=""):
             codes = tile([P, P], U32, name + "_codes", behind)
@@ -185,7 +182,7 @@ def tile_attend_pqvalues_kernel(tc, query, keys_words, keys_scales, vbook, size,
 
         def woven_from(bank, name, behind=""):
             woven = tile([P, P * PACK], BF16, name, behind)
-            weave(bank, by_half(woven))
+            weave(bank, woven)
             return woven
 
         raw0 = scalar_gather(0, HALF_I, HALF_I, "raw0", "first_ident")
@@ -236,7 +233,7 @@ def tile_attend_pqvalues_kernel(tc, query, keys_words, keys_scales, vbook, size,
         plain_round(rounded3, prod3, 0)
         woven1 = woven_from(bank1, "woven1", "book3")
 
-        w_bank = ps.tile([P, PAIRS, Q], F32, name="w_bank", tag="bank_f")
+        w_bank = ps.tile([P, Q, PAIRS], F32, name="w_bank", tag="bank_f")
         for u in range(PAIRS):
             weights = tile([P, P * PAIR], BF16, "weights%d" % u)
             nc.vector.scalar_tensor_tensor(
@@ -247,7 +244,7 @@ def tile_attend_pqvalues_kernel(tc, query, keys_words, keys_scales, vbook, size,
                 ALU.mult,
                 ALU.mult,
             )
-            nc.tensor.transpose(w_bank[:, u, :], weights.bitcast(F32), ident)
+            nc.tensor.transpose(w_bank[:, :, u], weights.bitcast(F32), ident)
         for u in range(PAIRS):
             vector_round(rounded3, raw3, HALF_I, slice(u, u + 1))
         bank3 = turn(rounded3, "v3_bank", "bank_e")
@@ -256,8 +253,8 @@ def tile_attend_pqvalues_kernel(tc, query, keys_words, keys_scales, vbook, size,
         woven3 = tile([P, P * PACK], BF16, "woven3")
         for h in range(HALVES):
             nc.scalar.copy(
-                by_half(woven3)[:, h, :].bitcast(F32).rearrange("n (r u) -> n r u", u=PAIRS),
-                bank3[:, :, h * HALF_P : (h + 1) * HALF_P].rearrange("n u r -> n r u"),
+                by_half(woven3)[:, h, :].bitcast(F32),
+                bank3[:, h * HALF_P : (h + 1) * HALF_P, :].rearrange("n r u -> n (r u)"),
             )
         woven2 = tile([P, P * PACK], BF16, "woven2", "probs")
         nc.vector.tensor_tensor(

@@ -60,10 +60,10 @@ def tile_attend_pqvalues_kernel(tc, query, keys_words, keys_scales, vbook, size,
         ident = tile([P, P], F32, "ident")
 
         nc.vector.memset(key_bytes.bitcast(I32), 0)
-        distance = tile([P, P], F32, "distance", room_kib=20)
-        nc.gpsimd.iota(distance, [[1, P]], base=0, channel_multiplier=-1, allow_small_or_imprecise_dtypes=True)
+        zeros = tile([P, P], F32, "zeros", room_kib=20)
+        nc.gpsimd.memset(zeros, 0.0)
         first_ident = tile([P, P], F32, "first_ident", room_kib=12)
-        nc.vector.tensor_scalar(first_ident, distance, 0.0, None, ALU.is_equal)
+        nc.gpsimd.affine_select(first_ident, zeros, [[-1, P]], ALU.not_equal, 1.0, base=0, channel_multiplier=1)
         nc.vector.tensor_copy(ident, first_ident)
 
         book_rows = vbook.rearrange("(p j) c -> j p c", j=PACK)
@@ -83,12 +83,12 @@ def tile_attend_pqvalues_kernel(tc, query, keys_words, keys_scales, vbook, size,
         size_col = tile([P, PACK], F32, "size_col")
         nc.sync.dma_start(size_col, size.rearrange("o (p t) -> p (o t)", t=PACK))
         nc.sync.dma_start(key_bytes[0:P:BLOCK, :].bitcast(I32), keys_scales[0].bitcast(I32))
-        load_book("distance")
-        key_words = tile([P, T], I32, "key_words", "distance")
+        load_book("zeros")
+        key_words = tile([P, T], I32, "key_words", "zeros")
         nc.sync.dma_start(key_words, keys_words[0].rearrange("p n t -> p (n t)").bitcast(I32))
-        load_book("distance")
+        load_book("zeros")
 
-        picked_bytes = tile([P, I], U8, "picked_bytes", "distance", 1)
+        picked_bytes = tile([P, I], U8, "picked_bytes", "zeros", 1)
         nc.vector.tensor_copy(picked_bytes, key_bytes.indirect(key_list[:]))
         key_scales = tile([P, I], U8, "key_scales")
         nc.vector.tensor_copy(key_scales.bitcast(I32), picked_bytes.bitcast(I32))

from contextlib import ExitStack

import concourse.mybir as mybir

D, T, I, C, Q, E = 512, 2048, 512, 1024, 128, 512
FLOPS = 2 * Q * I * D + 2 * Q * I * E

F32 = mybir.dt.float32
BF16 = mybir.dt.bfloat16
I32 = mybir.dt.int32
U32 = mybir.dt.uint32
U16 = mybir.dt.uint16
U8 = mybir.dt.uint8
FP8X4 = mybir.dt.float8_e4m3fn_x4
ALU = mybir.AluOpType
ACT = mybir.ActivationFunctionType
AXIS = mybir.AxisListType

P = 128
PACK = 4
PAIR = 2
PAIRS = PACK // PAIR
GROUP = 16
BLOCK = 8
QUADRANT = 32
HALVES = 2
HALF_P = P // HALVES
HALF_I = I // 2
SHORT = 128
KIB = 1024
ROW_OF_BOOK = (0, 2, 1, 3)


def tile_attend_pqvalues_kernel(tc, query, keys_words, keys_scales, vbook, size, vsc, offs, offs2, out):
    nc = tc.nc
    with ExitStack() as ctx:
        sb = ctx.enter_context(tc.tile_pool(name="sb", bufs=1))
        placed = ctx.enter_context(tc.tile_pool(name="placed", bufs=1))
        ps = ctx.enter_context(tc.psum_pool(name="ps", bufs=1))
        free = {"": (0, 200 * KIB)}

        def tile(shape, dtype, name, behind="", room_kib=0):
            width = 4 if dtype in (F32, I32, U32) else 2 if dtype == BF16 else 1
            columns = 1
            for extent in shape[1:]:
                columns = columns * extent
            span = max(room_kib * KIB, -(-columns * width // 64) * 64)
            start, end = free[behind]
            assert start + span <= end
            free[behind] = (start + span, end)
            free[name] = (start, start + span)
            if room_kib == 0:
                return placed.tile(shape, dtype, name=name, offset=start, align_bytes=64)[:]
            assert len(shape) == 2
            return placed.tile([P, span // width], dtype, name=name, offset=start, align_bytes=64)[:, 0:columns]

        key_list = sb.tile([P, I // GROUP], U16, name="key_list")
        code_lists = sb.tile([P, I // GROUP], U16, name="code_lists")
        key_bytes = tile([P, T], U8, "key_bytes", room_kib=4)
        ident = tile([P, P], F32, "ident")

        nc.vector.memset(key_bytes.bitcast(I32), 0)
        zeros = tile([P, P], F32, "zeros", room_kib=20)
        nc.gpsimd.memset(zeros, 0.0)
        first_ident = tile([P, P], F32, "first_ident", room_kib=12)
        nc.gpsimd.affine_select(first_ident, zeros, [[-1, P]], ALU.not_equal, 1.0, base=0, channel_multiplier=1)
        nc.vector.tensor_copy(ident, first_ident)

        book_rows = vbook.rearrange("(p j) c -> j p c", j=PACK)
        books = []

        def load_book(behind):
            book = tile([P, C], F32, "book%d" % len(books), behind)
            nc.sync.dma_start(book, book_rows[ROW_OF_BOOK[len(books)]])
            books.append(book)

        q_raw = tile([P, PACK * Q], F32, "q_raw")
        nc.scalar.dma_start(q_raw.rearrange("p (j q) -> p j q", j=PACK), query.rearrange("(p j) q -> p j q", j=PACK))
        vsc_col = tile([P, PACK], F32, "vsc_col")
        nc.sync.dma_start(vsc_col, vsc.rearrange("(p t) o -> p (t o)", t=PACK))
        nc.sync.dma_start(key_list[:], offs)
        nc.sync.dma_start(code_lists[:], offs2)
        size_col = tile([P, PACK], F32, "size_col")
        nc.sync.dma_start(size_col, size.rearrange("o (p t) -> p (o t)", t=PACK))
        nc.sync.dma_start(key_bytes[0:P:BLOCK, :].bitcast(I32), keys_scales[0].bitcast(I32))
        load_book("zeros")
        key_words = tile([P, T], I32, "key_words", "zeros")
        nc.sync.dma_start(key_words, keys_words[0].rearrange("p n t -> p (n t)").bitcast(I32))
        load_book("zeros")

        picked_bytes = tile([P, I], U8, "picked_bytes", "zeros", 1)
        nc.vector.tensor_copy(picked_bytes, key_bytes.indirect(key_list[:]))
        key_scales = tile([P, I], U8, "key_scales")
        nc.vector.tensor_copy(key_scales.bitcast(I32), picked_bytes.bitcast(I32))
        for r in range(1, PACK):
            nc.sync.dma_start(
                key_scales[r:P:QUADRANT, :].bitcast(I32), picked_bytes[BLOCK * r : P : QUADRANT, :].bitcast(I32)
            )

        def spread(col, name, tag, identity):
            bank = ps.tile([P, PAIRS, P, PAIR], F32, name=name, tag=tag)
            for t in range(PACK):
                nc.tensor.transpose(bank[:, t // PAIR, :, t % PAIR], col[:, t : t + 1].to_broadcast([P, P]), identity)
            return bank

        vsc_bank = spread(vsc_col, "vsc_bank", "bank_a", first_ident)
        load_book("first_ident")
        load_book("first_ident")

        q_woven = tile([P, Q * PACK], BF16, "q_woven")
        nc.scalar.copy(q_woven.rearrange("p (q j) -> p q j", j=PACK), q_raw.rearrange("p (j q) -> p q j", j=PACK))
        vsc_low = tile([P, HALF_I], F32, "vsc_low", "", 3)
        nc.scalar.copy(
            vsc_low.rearrange("p (n u s) -> p n u s", u=PAIRS, s=PAIR),
            vsc_bank[:, :, 0 : HALF_I // PACK, :].rearrange("p u n s -> p n u s"),
        )

        def by_pair(columns):
            return columns.rearrange("p (n u s) -> p u n s", u=PAIRS, s=PAIR)

        def listed(j, first, count):
            return books[j].indirect(code_lists[:, first // GROUP : (first + count) // GROUP])

        def slots(rounded, first, count):
            return rounded[:, :, first // PACK : (first + count) // PACK, :]

        def vector_gather(j, first, factors, name, behind="", room_kib=0):
            count = factors.shape[1]
            prod = tile([P, count], F32, name, behind, room_kib)
            nc.vector.tensor_tensor(prod, listed(j, first, count), factors, ALU.mult)
            return prod

        def scalar_gather(j, first, count, name, behind="", room_kib=0):
            raw = tile([P, count], F32, name, behind, room_kib)
            nc.scalar.activation(raw, listed(j, first, count), ACT.Copy)
            return raw

        def plain_round(rounded, prod, first, copy=nc.scalar.copy):
            copy(slots(rounded, first, prod.shape[1]), by_pair(prod))

        def vector_round(rounded, raw, first, pairs=slice(0, PAIRS)):
            count = raw.shape[1]
            nc.vector.tensor_tensor(
                slots(rounded, first, count)[:, pairs],
                by_pair(raw)[:, pairs],
                slots(vsc_bank, first, count)[:, pairs],
                ALU.mult,
            )

        def turn(rounded, name, tag):
            bank = ps.tile([P, P, PAIRS], F32, name=name, tag=tag)
            for u in range(PAIRS):
                words = rounded[:, u].rearrange("p n s -> p (n s)").bitcast(F32)
                nc.tensor.transpose(bank[:, :, u], words, ident)
            return bank

        def weave(bank, woven, copy=nc.scalar.copy):
            copy(woven.bitcast(F32), bank[:].rearrange("n p u -> n (p u)"))

        def quantise(woven, name, behind=""):
            codes = tile([P, P], U32, name + "_codes", behind)
            scales = tile([P, P], U8, name + "_scales")
            nc.vector.quantize_mx(out=codes.bitcast(FP8X4), scales=scales, in_=woven)
            return codes, scales

        def by_half(woven):
            return woven.rearrange("n (h r) -> n h r", h=HALVES)

        pair_shape = [P, PAIRS, P, PAIR]

        def value_tiles(name, behind):
            codes = tile([P, HALVES, PAIR, HALF_P], U32, name + "_codes", behind)
            scales = tile([P, HALVES, PAIR, HALF_P], U8, name + "_scales")
            return codes, scales

        def quantise_book(pair, place, woven):
            codes, scales = pair
            for h in range(HALVES):
                nc.vector.quantize_mx(
                    out=codes[:, h, place, :].bitcast(FP8X4), scales=scales[:, h, place, :], in_=by_half(woven)[:, h, :]
                )

        def woven_from(bank, name, behind=""):
            woven = tile([P, P * PACK], BF16, name, behind)
            weave(bank, woven)
            return woven

        raw0 = scalar_gather(0, HALF_I, HALF_I, "raw0", "first_ident")
        prod0 = vector_gather(0, 0, vsc_low, "prod0", "key_bytes")
        rounded0 = tile(pair_shape, BF16, "rounded0", "key_bytes")
        plain_round(rounded0, prod0, 0)
        vector_round(rounded0, raw0, HALF_I)
        bank0 = turn(rounded0, "v0_bank", "bank_b")
        q_codes, q_scales = quantise(q_woven, "q", "key_bytes")

        picked_words = tile([P, I], U32, "picked_words", "book0")
        nc.vector.tensor_copy(picked_words, key_words.bitcast(U32).indirect(key_list[:]))
        scores = ps.tile([P, I], F32, name="scores", tag="bank_e")
        nc.tensor.matmul_mx(
            out=scores[:],
            lhsT=q_codes.bitcast(FP8X4),
            lhsT_scale=q_scales,
            rhs=picked_words.bitcast(FP8X4),
            rhs_scale=key_scales,
            start=True,
            stop=True,
        )
        woven0 = woven_from(bank0, "woven0")
        prod1 = vector_gather(1, 0, vsc_low, "prod1", "key_words")
        raw1 = scalar_gather(1, HALF_I, HALF_I, "raw1", "raw0")
        rounded1 = tile(pair_shape, BF16, "rounded1", "picked_bytes")
        vector_round(rounded1, raw1, HALF_I)
        neg_max = tile([P, 1], F32, "neg_max")
        nc.vector.tensor_reduce(neg_max, scores[:], AXIS.X, ALU.max, negate=True)
        plain_round(rounded1, prod1, 0, nc.vector.tensor_copy)
        size_bank = spread(size_col, "size_bank", "bank_c", ident)
        bank1 = turn(rounded1, "v1_bank", "bank_b")

        raw2 = scalar_gather(2, 0, I, "raw2")
        bank2 = ps.tile([P, P, PACK], F32, name="v2_bank", tag="bank_d")
        for t in range(PACK):
            nc.tensor.transpose(bank2[:, :, t], raw2[:, t:I:PACK], ident)
        probs = tile(pair_shape, F32, "probs", "book2")
        row_sum = tile([P, 1], F32, "row_sum", "", 1)
        nc.scalar.activation(probs, by_pair(scores[:]), ACT.Exp, bias=neg_max, accum_out=row_sum)
        raw3 = scalar_gather(3, HALF_I, HALF_I, "raw3")
        prod3 = vector_gather(3, 0, vsc_low, "prod3")
        inv_sum = tile([P, 1], F32, "inv_sum", "vsc_low")
        nc.vector.reciprocal(inv_sum, row_sum)
        even = value_tiles("even", "vsc_low")
        quantise_book(even, 0, woven0)
        rounded3 = tile(pair_shape, BF16, "rounded3", "row_sum")
        plain_round(rounded3, prod3, 0)
        woven1 = woven_from(bank1, "woven1", "book3")

        w_bank = ps.tile([P, Q, PAIRS], F32, name="w_bank", tag="bank_f")
        for u in range(PAIRS):
            weights = tile([P, P * PAIR], BF16, "weights%d" % u)
            nc.vector.scalar_tensor_tensor(
                weights.rearrange("q (n s) -> q n s", s=PAIR),
                probs[:, u],
                inv_sum,
                size_bank[:, u],
                ALU.mult,
                ALU.mult,
            )
            nc.tensor.transpose(w_bank[:, :, u], weights.bitcast(F32), ident)
        for u in range(PAIRS):
            vector_round(rounded3, raw3, HALF_I, slice(u, u + 1))
        bank3 = turn(rounded3, "v3_bank", "bank_e")

        w_woven = woven_from(w_bank, "w_woven")
        woven3 = tile([P, P * PACK], BF16, "woven3")
        for h in range(HALVES):
            nc.scalar.copy(
                by_half(woven3)[:, h, :].bitcast(F32),
                bank3[:, h * HALF_P : (h + 1) * HALF_P, :].rearrange("n r u -> n (r u)"),
            )
        woven2 = tile([P, P * PACK], BF16, "woven2", "probs")
        nc.vector.tensor_tensor(
            woven2.rearrange("n (c t) -> n c t", t=PACK),
            bank2[:],
            vsc_col.unsqueeze(1).to_broadcast([P, P, PACK]),
            ALU.mult,
        )
        odd = value_tiles("odd", "probs")
        w_codes, w_scales = quantise(w_woven, "w")
        quantise_book(even, 1, woven2)
        quantise_book(odd, 0, woven1)
        quantise_book(odd, 1, woven3)

        sums = [ps.tile([P, PACK, HALF_P], F32, name="sums%d" % h) for h in range(HALVES)]
        for number, (codes, scales) in enumerate((even, odd)):
            these = slice(number * PAIR, (number + 1) * PAIR)
            for h in range(HALVES):
                nc.tensor.matmul_mx(
                    out=sums[h][:, these, :].rearrange("q j r -> q (j r)"),
                    lhsT=w_codes.bitcast(FP8X4),
                    lhsT_scale=w_scales,
                    rhs=codes[:, h].rearrange("n j r -> n (j r)").bitcast(FP8X4),
                    rhs_scale=scales[:, h].rearrange("n j r -> n (j r)"),
                    start=True,
                    stop=True,
                )
        for h in range(HALVES):
            result = tile([P, E // HALVES], F32, "result%d" % h)
            copy = (nc.vector.tensor_copy, nc.scalar.copy)[h]
            copy(
                result.rearrange("q (c i j) -> q c j i", i=PAIR, j=PACK),
                sums[h][:].rearrange("q j (c i) -> q c j i", i=PAIR),
            )
            queue = (nc.sync, nc.scalar)[h]
            queue.dma_start(out[:, h * (E // HALVES) : (h + 1) * (E // HALVES)], result)
